import numpy as np
import ml_dtypes


def mxq(x, axis, fmt="e4m3"):
    dtype, down = {"e4m3": (ml_dtypes.float8_e4m3fn, 7), "e5m2": (ml_dtypes.float8_e5m2, 14)}[fmt]
    v = np.moveaxis(np.asarray(x, np.float32).astype(ml_dtypes.bfloat16).astype(np.float64), axis, -1)
    blocks = v.reshape(v.shape[:-1] + (-1, 32))
    amax = np.abs(blocks).max(-1, keepdims=True)
    byte = np.maximum(np.where(amax > 0, np.frexp(amax)[1] - 1 + 127, 0) - down, 1)
    scale = np.exp2(byte - 127.0)
    codes = (blocks / scale).astype(np.float32).astype(dtype).astype(np.float64)
    return np.moveaxis((codes * scale).reshape(v.shape), -1, axis)


WIDE = False


def mx_kscale(k):
    if not WIDE:
        return np.ones(k)
    levels = np.array([10, -10, 5, -5, 0])
    if k % 512:
        return np.exp2(np.random.permutation(np.resize(levels, k // 32))).repeat(32)
    a = np.empty((k // 512, 16))
    for p in range(k // 512):
        a[p, :8] = np.random.permutation(np.resize(levels, 8))
        for g in range(8):
            far = levels[np.abs(levels - a[p, g]) >= 10]
            a[p, g + 8] = far[np.random.randint(len(far))]
    return np.exp2(a.ravel()).repeat(32)


BF16 = ml_dtypes.bfloat16


def bf(x):
    return np.asarray(x, np.float32).astype(BF16)


def f64(x):
    return np.asarray(x).astype(np.float64)

def planes(Y):
    n, m = Y.shape
    b = f64(bf(Y)).reshape(n // 32, 32, m)
    amax = np.abs(b).max(1)
    byte = np.clip(np.where(amax > 0, np.frexp(amax)[1] - 1 + 127 - 7, 1), 1, 254)
    codes = (b * np.exp2(127.0 - byte)[:, None, :]).reshape(n, m).astype(np.float32).astype(ml_dtypes.float8_e4m3fn).view(np.uint8)
    words = codes.reshape(n // 512, 128, 4, m).transpose(0, 1, 3, 2)
    return np.ascontiguousarray(words), np.ascontiguousarray(byte.astype(np.uint8).reshape(n // 512, 16, m))


N, M, D, F = 1024, 1024, 512, 1024


def setup_inputs():
    s, u = mx_kscale(D), mx_kscale(M)
    c = np.random.uniform(0.4, 1.2, (N, 1))
    return {"q": bf(np.random.standard_normal((N, D)) * c * s),
            "k": bf(np.random.standard_normal((M, D)) / s),
            "a": bf(np.random.standard_normal(N) * 0.4),
            "t": bf(np.random.uniform(0.0, 2.0, (N, M)) * (M / N)),
            "g": bf((1.0 + 0.1 * np.random.standard_normal(M)) * u),
            "v": bf(np.random.standard_normal((M, F)) * np.sqrt(N / M) / u[:, None])}


def lse(x, axis):
    top = x.max(axis=axis, keepdims=True)
    return top + np.log(np.sum(np.exp(x - top), axis=axis, keepdims=True))


def core(q, k, a, t, g, v):
    s = (mxq(f64(q), 1, "e4m3") @ mxq(f64(k), 1, "e4m3").T) / np.sqrt(D)
    f = lse(s, 1)
    b = s - f + f64(a)[:, None]
    h = lse(b, 0)
    p = M * np.exp(b - h)
    r = (p - f64(t)) * f64(g)[None, :]
    return (mxq(r, 1, "e4m3") @ mxq(f64(v), 0, "e4m3")) / np.sqrt(M)


def reference(q, k, a, t, g, v):
    R_out = core(q, k, a, t, g, v)
    words, scales = planes(R_out)
    return R_out, words, scales

@@ -1,0 +1,476 @@
+import math
+from contextlib import ExitStack
+
+import concourse.mybir as mybir
+from concourse.masks import make_identity
+
+N, M, D, F = 1024, 1024, 512, 1024
+FLOPS = 2 * N * M * D + 2 * N * M * F
+
+F32 = mybir.dt.float32
+BF16 = mybir.dt.bfloat16
+U32 = mybir.dt.uint32
+I32 = mybir.dt.int32
+U8 = mybir.dt.uint8
+FP8X4 = mybir.dt.float8_e4m3fn_x4
+ALU = mybir.AluOpType
+ACT = mybir.ActivationFunctionType
+AX = mybir.AxisListType
+
+P = 128
+W = 512
+SCALE = 1.0 / math.sqrt(D)
+RAW = math.sqrt(D)
+
+
+def tile_sinkhorninverseotresidualpull_x1_kernel(tc, q, k, a, t, g, v, out_0, out_1, out_2):
+    nc = tc.nc
+    with ExitStack() as ctx:
+        keep = ctx.enter_context(tc.tile_pool(name="keep", bufs=1))
+        work = ctx.enter_context(tc.tile_pool(name="work", bufs=4))
+        psum = ctx.enter_context(tc.psum_pool(name="psum", bufs=4))
+        ctx.enter_context(tc.manual_schedule())
+
+        k_raw, q_raw, v_raw, t_raw = [], [], [], []
+        for G in range(2):
+            for dst, src, name in ((k_raw, k, "k_raw"), (q_raw, q, "q_raw")):
+                raw = keep.tile([P, 4, D], BF16, name=name + str(G))
+                rows = src[W * G : W * G + W, :].rearrange("(p t) d -> p t d", t=4)
+                for c in range(2):
+                    nc.sync.dma_start(out=raw[:, 2 * c : 2 * c + 2, :], in_=rows[:, 2 * c : 2 * c + 2, :])
+                dst.append(raw)
+        a_bf = keep.tile([P, 2, 4], BF16, name="a_bf")
+        g_bf = keep.tile([P, 2, 4], BF16, name="g_bf")
+        nc.sync.dma_start(out=a_bf[:], in_=a.rearrange("(g p t) -> p g t", g=2, t=4))
+        nc.sync.dma_start(out=g_bf[:], in_=g.rearrange("(g p t) -> p g t", g=2, t=4))
+        for dst, src, name in ((v_raw, v, "v_raw"), (t_raw, t, "t_raw")):
+            for G in range(2):
+                raw = keep.tile([P, 4, 1024], BF16, name=name + str(G))
+                nc.sync.dma_start(out=raw[:], in_=src[W * G : W * G + W, :].rearrange("(p t) d -> p t d", t=4))
+                dst.append(raw)
+
+        ident = keep.tile([P, P], F32, name="ident")
+        make_identity(nc, ident[:])
+        warm = keep.tile([P, 2], F32, name="warm")
+        nc.vector.memset(warm[:], 0.0)
+        nc.scalar.activation(out=warm[:, 1:2], in_=warm[:, 0:1], func=ACT.Exp)
+
+        k_codes = keep.tile([P, M], U32, name="k_codes", align_bytes=64)
+        k_scales = keep.tile([P, M], U8, name="k_scales", align_bytes=64)
+        q_codes = keep.tile([P, N], U32, name="q_codes", align_bytes=64)
+        q_scales = keep.tile([P, N], U8, name="q_scales", align_bytes=64)
+        v_codes = [keep.tile([P, F], U32, name="v_codes" + str(G), align_bytes=64) for G in range(2)]
+        v_scales = [keep.tile([P, F], U8, name="v_scales" + str(G), align_bytes=64) for G in range(2)]
+        r_codes = [keep.tile([P, N], U32, name="r_codes" + str(G), align_bytes=64) for G in range(2)]
+        r_scales = [keep.tile([P, N], U8, name="r_scales" + str(G), align_bytes=64) for G in range(2)]
+
+        def bank(tag):
+            return psum.tile([P, W], F32, name="bank_" + tag, tag=tag)
+
+        def quad_tile(name):
+            return work.tile([P, W, 4], BF16, name=name, tag="quads", bufs=4, align_bytes=64)
+
+        def quantize(quads, codes, scales, cols):
+            nc.vector.quantize_mx(
+                out=codes[:, cols].bitcast(FP8X4),
+                scales=scales[:, cols],
+                in_=quads.rearrange("p c t -> p (c t)"),
+            )
+
+        def turn_rows(raw, quads, slot0, tag, copy):
+            words = raw[:].bitcast(F32)
+            xt = bank(tag)
+            xt4 = xt[:].rearrange("p (s u r) -> p s u r", s=2, u=2)
+            for s in range(2):
+                for u in range(2):
+                    nc.tensor.transpose(xt4[:, s, u, :], words[:, slot0 + s, u : D // 2 : 2], ident[:])
+            dst = quads[:, P * slot0 : P * (slot0 + 2), :].bitcast(F32).rearrange("p (s r) u -> p s r u", s=2)
+            copy(dst, xt4.rearrange("p s u r -> p s r u"))
+
+        def s_copy(dst, src):
+            nc.scalar.copy(out=dst, in_=src)
+
+        def v_copy(dst, src):
+            nc.vector.tensor_copy(out=dst, in_=src)
+
+        kq = [quad_tile("k_quads") for G in range(2)]
+        qq = [quad_tile("q_quads") for G in range(2)]
+
+        def quantize_k(G):
+            quantize(kq[G][:], k_codes, k_scales, slice(W * G, W * G + W))
+
+        def quantize_q(G, c):
+            quantize(qq[G][:, 256 * c : 256 * c + 256, :], q_codes, q_scales, slice(W * G + 256 * c, W * G + 256 * c + 256))
+
+        v_quads = []
+        for G in range(2):
+            vq = keep.tile([P, F, 4], BF16, name="v_quads" + str(G), align_bytes=64)
+            for c in range(2):
+                cols = slice(W * c, W * c + W)
+                nc.gpsimd.tensor_scalar(
+                    out=vq[:, cols, :], in0=v_raw[G][:, :, cols].rearrange("p t f -> p f t"),
+                    scalar1=1.0, scalar2=0.0, op0=ALU.mult, op1=ALU.add,
+                )
+            v_quads.append(vq)
+
+        def quantize_v(i):
+            G, c = divmod(i, 2)
+            cols = slice(W * c, W * c + W)
+            quantize(v_quads[G][:, cols, :], v_codes[G], v_scales[G], cols)
+
+        TAGS = ("x", "y")
+        maxes = keep.tile([P, 8, 2], F32, name="maxes")
+        shift = keep.tile([P, 8], F32, name="shift")
+        z2 = keep.tile([P, 8, 2], F32, name="z2")
+
+        def score_bank(n, h):
+            ps = bank(TAGS[h])
+            nc.tensor.matmul_mx(
+                out=ps[:],
+                lhsT=q_codes[:, P * n : P * n + P].bitcast(FP8X4), lhsT_scale=q_scales[:, P * n : P * n + P],
+                rhs=k_codes[:, W * h : W * h + W].bitcast(FP8X4), rhs_scale=k_scales[:, W * h : W * h + W],
+                start=True, stop=True,
+            )
+            return ps
+
+        def row_max(n, h, ps):
+            nc.vector.reduce_max(out=maxes[:, n, h : h + 1], in_=ps[:], axis=AX.X)
+
+        def row_shift(n):
+            nc.vector.tensor_scalar(
+                out=shift[:, n : n + 1], in0=maxes[:, n, 0:1], scalar1=maxes[:, n, 1:2], scalar2=-SCALE,
+                op0=ALU.max, op1=ALU.mult,
+            )
+
+        def row_exp(n, h, ps):
+            junk = work.tile([P, W], BF16, name="junk", tag="junk", bufs=2)
+            nc.scalar.activation(
+                out=junk[:], in_=ps[:], func=ACT.Exp, bias=shift[:, n : n + 1], scale=SCALE,
+                accum_out=z2[:, n, h : h + 1],
+            )
+
+        turn_rows(k_raw[0], kq[0], 0, "x", s_copy)
+        turn_rows(k_raw[0], kq[0], 2, "x", v_copy)
+        turn_rows(q_raw[0], qq[0], 0, "y", s_copy)
+        quantize_k(0)
+        quantize_q(0, 0)
+        turn_rows(q_raw[0], qq[0], 2, "y", s_copy)
+        turn_rows(k_raw[1], kq[1], 0, "y", s_copy)
+        ps = {}
+        for n in range(2):
+            ps[n, 0] = score_bank(n, 0)
+            row_max(n, 0, ps[n, 0])
+        quantize_q(0, 1)
+        turn_rows(k_raw[1], kq[1], 2, "y", s_copy)
+        turn_rows(q_raw[1], qq[1], 0, "y", s_copy)
+        for n in range(2, 4):
+            ps[n, 0] = score_bank(n, 0)
+        quantize_k(1)
+        for n in range(2):
+            ps[n, 1] = score_bank(n, 1)
+        row_max(2, 0, ps[2, 0])
+        row_max(0, 1, ps[0, 1])
+        row_shift(0)
+        row_exp(0, 0, ps[0, 0])
+        row_exp(0, 1, ps[0, 1])
+        row_max(1, 1, ps[1, 1])
+        row_shift(1)
+        turn_rows(q_raw[1], qq[1], 2, "y", s_copy)
+        row_max(3, 0, ps[3, 0])
+        row_exp(1, 0, ps[1, 0])
+        row_exp(1, 1, ps[1, 1])
+        for n in range(2, 8):
+            ps[n, 1] = score_bank(n, 1)
+            if n > 3:
+                row_max(n, 0, ps[n, 0])
+            row_max(n, 1, ps[n, 1])
+            if n < 4:
+                quantize_q(1, n - 2)
+            row_shift(n)
+            if n < 6:
+                ps[n + 2, 0] = score_bank(n + 2, 0)
+            for h in range(2):
+                row_exp(n, h, ps[n, h])
+        g_f32 = keep.tile([P, 2, 1, 4], F32, name="g_f32")
+        nc.vector.tensor_copy(out=g_f32[:, :, 0, :], in_=g_bf[:])
+
+        a_shift = keep.tile([P, 8], F32, name="a_shift")
+        a_raw = keep.tile([P, 8], F32, name="a_raw")
+        z = keep.tile([P, 8], F32, name="z")
+        ln_z = keep.tile([P, 8], F32, name="ln_z")
+        c_row = keep.tile([P, 8], F32, name="c_row")
+        b_rows = [keep.tile([P, M], F32, name="b_rows" + str(n)) for n in range(8)]
+        acc = [keep.tile([P, W], F32, name="acc" + str(h)) for h in range(2)]
+
+        def b_scalar(n, h):
+            nc.scalar.activation(
+                out=b_rows[n][:, W * h : W * h + W], in_=ps[n, h][:], func=ACT.Identity,
+                bias=c_row[:, n : n + 1], scale=SCALE,
+            )
+
+        def b_vector(n, h):
+            nc.vector.tensor_scalar(
+                out=b_rows[n][:, W * h : W * h + W], in0=ps[n, h][:], scalar1=SCALE, scalar2=c_row[:, n : n + 1],
+                op0=ALU.mult, op1=ALU.add,
+            )
+
+        def col_max(n, h):
+            if n == 0:
+                nc.vector.tensor_scalar(
+                    out=acc[h][:], in0=ps[n, h][:], scalar1=a_raw[:, 0:1], scalar2=None, op0=ALU.add
+                )
+            else:
+                nc.vector.scalar_tensor_tensor(
+                    out=acc[h][:], in0=ps[n, h][:], scalar=a_raw[:, n : n + 1], in1=acc[h][:], op0=ALU.add, op1=ALU.max,
+                )
+
+        nc.vector.tensor_tensor(out=a_shift[:], in0=a_bf[:].rearrange("p g t -> p (g t)"), in1=shift[:], op=ALU.add)
+        quantize_v(0)
+        nc.vector.tensor_scalar(out=a_raw[:], in0=a_shift[:], scalar1=RAW, scalar2=None, op0=ALU.mult)
+        for n in range(8):
+            for h in range(2):
+                ps[n, h] = score_bank(n, h)
+            if n == 1:
+                nc.vector.tensor_tensor(out=z[:], in0=z2[:, :, 0], in1=z2[:, :, 1], op=ALU.add)
+                nc.scalar.activation(out=ln_z[:], in_=z[:], func=ACT.Ln)
+            if n == 2:
+                nc.vector.tensor_tensor(out=c_row[:], in0=a_shift[:], in1=ln_z[:], op=ALU.subtract)
+                for m in range(2):
+                    b_scalar(m, 0)
+                    b_scalar(m, 1)
+            col_max(n, 0)
+            col_max(n, 1)
+            if 2 <= n < 6:
+                b_scalar(n, 0)
+                b_scalar(n, 1)
+        b_scalar(6, 0)
+        b_scalar(6, 1)
+
+        h_raw = keep.tile([P, 8], F32, name="h_raw")
+        h_shift = keep.tile([P, 8], F32, name="h_shift")
+        h_banks = []
+        for h in range(2):
+            xt = bank("y")
+            for c in range(4):
+                nc.tensor.transpose(xt[:, P * c : P * c + P], acc[h][:, P * c : P * c + P], ident[:])
+            h_banks.append(xt)
+        b_vector(7, 0)
+        b_vector(7, 1)
+        for h in range(2):
+            nc.vector.reduce_max(
+                out=h_raw[:, 4 * h : 4 * h + 4], in_=h_banks[h][:].rearrange("p (c r) -> p c r", c=4), axis=AX.X,
+            )
+        nc.vector.tensor_scalar(out=h_shift[:], in0=h_raw[:], scalar1=-SCALE, scalar2=None, op0=ALU.mult)
+        quantize_v(2)
+
+        t_bank = {}
+
+        def turn_t(G, gi, u):
+            xt = bank("y")
+            for s in range(4):
+                words = t_raw[gi][:, s, :].bitcast(F32)
+                nc.tensor.transpose(xt[:, P * s : P * s + P], words[:, 256 * G + u : 256 * G + 256 : 2], ident[:])
+            t_bank[G, gi, u] = xt
+
+        e_cols = {}
+        ez = keep.tile([P, 8, 2], F32, name="ez")
+        ezs = keep.tile([P, 8], F32, name="ezs")
+        w_col = keep.tile([P, 8], F32, name="w_col")
+
+        def col_exp(J):
+            e = work.tile([P, N], F32, name="e_cols", tag="e_cols", bufs=8)
+            e_cols[J] = e
+            banks = []
+            for gi in range(2):
+                xt = bank("x")
+                for s in range(4):
+                    nc.tensor.transpose(
+                        xt[:, P * s : P * s + P], b_rows[4 * gi + s][:, P * J : P * J + P], ident[:]
+                    )
+                banks.append(xt)
+            for gi in range(2):
+                nc.scalar.activation(
+                    out=e[:, W * gi : W * gi + W], in_=banks[gi][:], func=ACT.Exp,
+                    bias=h_shift[:, J : J + 1], accum_out=ez[:, J, gi : gi + 1],
+                )
+
+        def col_sum(J):
+            nc.vector.tensor_scalar(
+                out=ezs[:, J : J + 1], in0=ez[:, J, 0:1], scalar1=ez[:, J, 1:2], scalar2=1.0 / M,
+                op0=ALU.add, op1=ALU.mult,
+            )
+
+        def col_weight(J):
+            nc.vector.reciprocal(out=w_col[:, J : J + 1], in_=ezs[:, J : J + 1])
+
+        residual = {}
+        r_quads = {}
+
+        def col_residual(J, gi):
+            G, s = divmod(J, 4)
+            if s == 0:
+                residual[G, gi] = work.tile([P, 4, W], F32, name="residual", tag="wide", bufs=4)
+            u, e = divmod(s, 2)
+            t_view = t_bank[G, gi, u][:].bitcast(BF16).rearrange("p (i e) -> p i e", e=2)[:, :, e]
+            nc.vector.scalar_tensor_tensor(
+                out=residual[G, gi][:, s, :], in0=e_cols[J][:, W * gi : W * gi + W], scalar=w_col[:, J : J + 1],
+                in1=t_view, op0=ALU.mult, op1=ALU.subtract,
+            )
+
+        def new_quads(G, gi):
+            r_quads[G, gi] = quad_tile("r_quads")
+
+        def gain_pool(G, gi, lo, hi):
+            nc.gpsimd.tensor_tensor(
+                out=r_quads[G, gi][:, lo:hi, :],
+                in0=residual[G, gi][:].rearrange("p t i -> p i t")[:, lo:hi, :],
+                in1=g_f32[:, G, :, :].to_broadcast([P, hi - lo, 4]), op=ALU.mult,
+            )
+
+        gained = {}
+
+        def gain_scalar(J, gi, lo, hi):
+            G, s = divmod(J, 4)
+            if s == 0:
+                gained[G, gi] = work.tile([P, 4, W], BF16, name="gained", tag="gained", bufs=2)
+            nc.scalar.activation(
+                out=gained[G, gi][:, s, lo:hi], in_=residual[G, gi][:, s, lo:hi], func=ACT.Copy,
+                scale=g_f32[:, G, 0, s : s + 1],
+            )
+
+        def gain_gather(G, gi, lo, hi):
+            nc.vector.tensor_copy(
+                out=r_quads[G, gi][:, lo:hi, :], in_=gained[G, gi][:].rearrange("p t i -> p i t")[:, lo:hi, :]
+            )
+
+        def quantize_r(G, gi):
+            quantize(r_quads[G, gi][:], r_codes[G], r_scales[G], slice(W * gi, W * gi + W))
+
+        turn_t(0, 0, 0)
+        col_exp(0)
+        turn_t(0, 0, 1)
+        col_exp(1)
+        turn_t(1, 0, 0)
+        turn_t(1, 0, 1)
+        FILL = {3: 0, 4: 1, 5: 2}
+        for J in range(8):
+            col_sum(J)
+            if J in FILL:
+                col_residual(FILL[J], 1)
+            col_weight(J)
+            col_residual(J, 0)
+            if J < 6:
+                col_exp(J + 2)
+            if J == 1:
+                turn_t(0, 1, 0)
+            if J == 3:
+                new_quads(0, 0)
+                for lo in range(0, W, 128):
+                    gain_pool(0, 0, lo, lo + 128)
+            if J == 4:
+                turn_t(0, 1, 1)
+        turn_t(1, 1, 0)
+        turn_t(1, 1, 1)
+        for J in range(4, 8):
+            gain_scalar(J, 0, 0, 384)
+        new_quads(1, 0)
+        gain_pool(1, 0, 384, W)
+        quantize_r(0, 0)
+        col_residual(3, 1)
+        gain_gather(1, 0, 0, 384)
+        new_quads(0, 1)
+        for lo in range(0, W, 128):
+            gain_pool(0, 1, lo, lo + 128)
+        quantize_r(1, 0)
+        for J in range(4, 8):
+            col_residual(J, 1)
+
+        out_wide = {}
+        out_quads = {}
+        out_scales = {}
+
+        def pull_bank(gi, f0, fw, s0, tag, copy):
+            step = W // fw
+            f_cols = slice(f0, f0 + fw)
+            if s0 == 0:
+                out_wide[gi, f0] = work.tile([P, 4, fw], F32, name="out_wide", tag="wide", bufs=4)
+            wide = out_wide[gi, f0]
+            ps = bank(tag)
+            for s in range(s0, s0 + step):
+                cols = slice(W * gi + P * s, W * gi + P * s + P)
+                for G in range(2):
+                    nc.tensor.matmul_mx(
+                        out=ps[:, fw * (s - s0) : fw * (s - s0) + fw],
+                        lhsT=r_codes[G][:, cols].bitcast(FP8X4), lhsT_scale=r_scales[G][:, cols],
+                        rhs=v_codes[G][:, f_cols].bitcast(FP8X4), rhs_scale=v_scales[G][:, f_cols],
+                        start=(G == 0), stop=(G == 1),
+                    )
+            copy(wide[:, s0 : s0 + step, :], ps[:].rearrange("p (t f) -> p t f", t=step))
+            if (s0 + step) % 2 == 0:
+                s_lo = s0 + step - 2
+                nc.sync.dma_start(
+                    out=out_0[W * gi : W * gi + W, :].rearrange("(p t) f -> p t f", t=4)[:, s_lo : s_lo + 2, f_cols],
+                    in_=wide[:, s_lo : s_lo + 2, :],
+                )
+
+        def s_out(dst, src):
+            nc.scalar.activation(out=dst, in_=src, func=ACT.Copy, scale=1.0 / math.sqrt(M))
+
+        def v_out(dst, src):
+            nc.vector.tensor_scalar(out=dst, in0=src, scalar1=1.0 / math.sqrt(M), scalar2=None, op0=ALU.mult)
+
+        def out_gather(gi, f0, fw):
+            quads = work.tile([P, fw, 4], BF16, name="out_quads", tag="quads", bufs=4, align_bytes=64)
+            out_quads[gi, f0] = quads
+            nc.vector.tensor_copy(out=quads[:], in_=out_wide[gi, f0][:].rearrange("p t f -> p f t"))
+
+        def out_quantize(gi, f0, fw):
+            if f0 == 0:
+                out_scales[gi] = keep.tile([P, F], U8, name="out_scales" + str(gi), align_bytes=64)
+            codes = work.tile([P, fw], U32, name="out_codes", tag="out_codes", bufs=5, align_bytes=64)
+            nc.vector.quantize_mx(
+                out=codes[:].bitcast(FP8X4), scales=out_scales[gi][:, f0 : f0 + fw],
+                in_=out_quads[gi, f0][:].rearrange("p f t -> p (f t)"),
+            )
+            nc.sync.dma_start(
+                out=out_1[gi].rearrange("p f t -> p (f t)")[:, 4 * f0 : 4 * (f0 + fw)].bitcast(I32),
+                in_=codes[:].bitcast(I32),
+            )
+            if f0 + fw == F:
+                for Q in range(4):
+                    nc.sync.dma_start(
+                        out=out_2[gi, 4 * Q : 4 * Q + 4, :].bitcast(I32),
+                        in_=out_scales[gi][32 * Q : 32 * Q + 4, :].bitcast(I32),
+                    )
+
+        gain_scalar(4, 1, 0, 256)
+        gain_scalar(5, 1, 0, 256)
+        for s in range(4):
+            pull_bank(0, 0, W, s, "x", s_out)
+            if s < 2:
+                gain_scalar(6 + s, 1, 0, 256)
+        quantize_v(1)
+        quantize_v(3)
+        new_quads(1, 1)
+        gain_pool(1, 1, 256, 384)
+        gain_pool(1, 1, 384, W)
+        gain_gather(1, 1, 0, 256)
+        quantize_r(0, 1)
+        for s in range(4):
+            pull_bank(0, W, W, s, "x", s_out)
+        out_gather(0, 0, W)
+        quantize_r(1, 1)
+        out_quantize(0, 0, W)
+        for s in range(4):
+            pull_bank(1, 0, W, s, "y", s_out)
+        out_gather(0, W, W)
+        for f0 in (W, 768):
+            for s0 in (0, 2):
+                pull_bank(1, f0, 256, s0, "x", s_out)
+        out_quantize(0, W, W)
+        out_gather(1, 0, W)
+        out_gather(1, W, 256)
+        out_quantize(1, 0, W)
+        out_gather(1, 768, 256)
+        out_quantize(1, W, 256)
+        out_quantize(1, 768, 256)

@@ -21,6 +21,7 @@ P = 128
 W = 512
 SCALE = 1.0 / math.sqrt(D)
 RAW = math.sqrt(D)
+PULL = 1.0 / math.sqrt(M)
 
 
 def tile_sinkhorninverseotresidualpull_x1_kernel(tc, q, k, a, t, g, v, out_0, out_1, out_2):
@@ -67,6 +68,9 @@ def tile_sinkhorninverseotresidualpull_x1_kernel(tc, q, k, a, t, g, v, out_0, ou
         def bank(tag):
             return psum.tile([P, W], F32, name="bank_" + tag, tag=tag)
 
+        def bank_pair(tag):
+            return [bank(tag), bank(tag)]
+
         def quad_tile(name):
             return work.tile([P, W, 4], BF16, name=name, tag="quads", bufs=4, align_bytes=64)
 
@@ -77,15 +81,14 @@ def tile_sinkhorninverseotresidualpull_x1_kernel(tc, q, k, a, t, g, v, out_0, ou
                 in_=quads.rearrange("p c t -> p (c t)"),
             )
 
-        def turn_rows(raw, quads, slot0, tag, copy):
+        def turn_rows(raw, quads, pair, c, copy):
             words = raw[:].bitcast(F32)
-            xt = bank(tag)
-            xt4 = xt[:].rearrange("p (s u r) -> p s u r", s=2, u=2)
+            xt = pair[c][:].rearrange("p (s u r) -> p s u r", s=2, u=2)
             for s in range(2):
                 for u in range(2):
-                    nc.tensor.transpose(xt4[:, s, u, :], words[:, slot0 + s, u : D // 2 : 2], ident[:])
-            dst = quads[:, P * slot0 : P * (slot0 + 2), :].bitcast(F32).rearrange("p (s r) u -> p s r u", s=2)
-            copy(dst, xt4.rearrange("p s u r -> p s r u"))
+                    nc.tensor.transpose(xt[:, s, u, :], words[:, 2 * c + s, u : D // 2 : 2], ident[:])
+            dst = quads[:, 256 * c : 256 * (c + 1), :].bitcast(F32).rearrange("p (s r) u -> p s r u", s=2)
+            copy(dst, xt.rearrange("p s u r -> p s r u"))
 
         def s_copy(dst, src):
             nc.scalar.copy(out=dst, in_=src)
@@ -93,8 +96,9 @@ def tile_sinkhorninverseotresidualpull_x1_kernel(tc, q, k, a, t, g, v, out_0, ou
         def v_copy(dst, src):
             nc.vector.tensor_copy(out=dst, in_=src)
 
+        qq1 = quad_tile("q_quads")
         kq = [quad_tile("k_quads") for G in range(2)]
-        qq = [quad_tile("q_quads") for G in range(2)]
+        qq = [quad_tile("q_quads"), qq1]
 
         def quantize_k(G):
             quantize(kq[G][:], k_codes, k_scales, slice(W * G, W * G + W))
@@ -102,39 +106,40 @@ def tile_sinkhorninverseotresidualpull_x1_kernel(tc, q, k, a, t, g, v, out_0, ou
         def quantize_q(G, c):
             quantize(qq[G][:, 256 * c : 256 * c + 256, :], q_codes, q_scales, slice(W * G + 256 * c, W * G + 256 * c + 256))
 
-        v_quads = []
-        for G in range(2):
-            vq = keep.tile([P, F, 4], BF16, name="v_quads" + str(G), align_bytes=64)
-            for c in range(2):
-                cols = slice(W * c, W * c + W)
+        v_quads = {}
+
+        def gather_v(i):
+            G, c = divmod(i, 2)
+            v_quads[i] = quad_tile("v_quads")
+            for lo in range(0, W, 128):
                 nc.gpsimd.tensor_scalar(
-                    out=vq[:, cols, :], in0=v_raw[G][:, :, cols].rearrange("p t f -> p f t"),
+                    out=v_quads[i][:, lo : lo + 128, :],
+                    in0=v_raw[G][:, :, W * c + lo : W * c + lo + 128].rearrange("p t f -> p f t"),
                     scalar1=1.0, scalar2=0.0, op0=ALU.mult, op1=ALU.add,
                 )
-            v_quads.append(vq)
 
         def quantize_v(i):
             G, c = divmod(i, 2)
-            cols = slice(W * c, W * c + W)
-            quantize(v_quads[G][:, cols, :], v_codes[G], v_scales[G], cols)
+            quantize(v_quads[i][:], v_codes[G], v_scales[G], slice(W * c, W * c + W))
 
         TAGS = ("x", "y")
         maxes = keep.tile([P, 8, 2], F32, name="maxes")
         shift = keep.tile([P, 8], F32, name="shift")
         z2 = keep.tile([P, 8, 2], F32, name="z2")
+        ps = {}
 
-        def score_bank(n, h):
-            ps = bank(TAGS[h])
+        def score(n, h):
+            if h == 0:
+                ps[n] = bank_pair(TAGS[n % 2])
             nc.tensor.matmul_mx(
-                out=ps[:],
+                out=ps[n][h][:],
                 lhsT=q_codes[:, P * n : P * n + P].bitcast(FP8X4), lhsT_scale=q_scales[:, P * n : P * n + P],
                 rhs=k_codes[:, W * h : W * h + W].bitcast(FP8X4), rhs_scale=k_scales[:, W * h : W * h + W],
                 start=True, stop=True,
             )
-            return ps
 
-        def row_max(n, h, ps):
-            nc.vector.reduce_max(out=maxes[:, n, h : h + 1], in_=ps[:], axis=AX.X)
+        def half_max(n, h):
+            nc.vector.reduce_max(out=maxes[:, n, h : h + 1], in_=ps[n][h][:], axis=AX.X)
 
         def row_shift(n):
             nc.vector.tensor_scalar(
@@ -142,135 +147,135 @@ def tile_sinkhorninverseotresidualpull_x1_kernel(tc, q, k, a, t, g, v, out_0, ou
                 op0=ALU.max, op1=ALU.mult,
             )
 
-        def row_exp(n, h, ps):
-            junk = work.tile([P, W], BF16, name="junk", tag="junk", bufs=2)
-            nc.scalar.activation(
-                out=junk[:], in_=ps[:], func=ACT.Exp, bias=shift[:, n : n + 1], scale=SCALE,
-                accum_out=z2[:, n, h : h + 1],
-            )
+        def row_exp(n):
+            for h in range(2):
+                junk = work.tile([P, W], BF16, name="junk", tag="junk", bufs=2)
+                nc.scalar.activation(
+                    out=junk[:], in_=ps[n][h][:], func=ACT.Exp, bias=shift[:, n : n + 1], scale=SCALE,
+                    accum_out=z2[:, n, h : h + 1],
+                )
 
-        turn_rows(k_raw[0], kq[0], 0, "x", s_copy)
-        turn_rows(k_raw[0], kq[0], 2, "x", v_copy)
-        turn_rows(q_raw[0], qq[0], 0, "y", s_copy)
+        pk0 = bank_pair("x")
+        pq0 = bank_pair("y")
+        pk1 = bank_pair("x")
+        pq1 = bank_pair("y")
+        turn_rows(k_raw[0], kq[0], pk0, 0, s_copy)
+        turn_rows(k_raw[0], kq[0], pk0, 1, v_copy)
+        turn_rows(q_raw[0], qq[0], pq0, 0, s_copy)
         quantize_k(0)
         quantize_q(0, 0)
-        turn_rows(q_raw[0], qq[0], 2, "y", s_copy)
-        turn_rows(k_raw[1], kq[1], 0, "y", s_copy)
-        ps = {}
-        for n in range(2):
-            ps[n, 0] = score_bank(n, 0)
-            row_max(n, 0, ps[n, 0])
+        turn_rows(q_raw[0], qq[0], pq0, 1, s_copy)
+        turn_rows(k_raw[1], kq[1], pk1, 0, s_copy)
+        score(0, 0)
+        score(1, 0)
+        half_max(0, 0)
         quantize_q(0, 1)
-        turn_rows(k_raw[1], kq[1], 2, "y", s_copy)
-        turn_rows(q_raw[1], qq[1], 0, "y", s_copy)
-        for n in range(2, 4):
-            ps[n, 0] = score_bank(n, 0)
+        half_max(1, 0)
+        turn_rows(k_raw[1], kq[1], pk1, 1, s_copy)
+        turn_rows(q_raw[1], qq[1], pq1, 0, s_copy)
         quantize_k(1)
+        turn_rows(q_raw[1], qq[1], pq1, 1, s_copy)
         for n in range(2):
-            ps[n, 1] = score_bank(n, 1)
-        row_max(2, 0, ps[2, 0])
-        row_max(0, 1, ps[0, 1])
+            score(n, 1)
+        half_max(0, 1)
         row_shift(0)
-        row_exp(0, 0, ps[0, 0])
-        row_exp(0, 1, ps[0, 1])
-        row_max(1, 1, ps[1, 1])
+        half_max(1, 1)
+        row_exp(0)
+        quantize_q(1, 0)
         row_shift(1)
-        turn_rows(q_raw[1], qq[1], 2, "y", s_copy)
-        row_max(3, 0, ps[3, 0])
-        row_exp(1, 0, ps[1, 0])
-        row_exp(1, 1, ps[1, 1])
+        row_exp(1)
+        quantize_q(1, 1)
+        for i in range(4):
+            gather_v(i)
         for n in range(2, 8):
-            ps[n, 1] = score_bank(n, 1)
-            if n > 3:
-                row_max(n, 0, ps[n, 0])
-            row_max(n, 1, ps[n, 1])
-            if n < 4:
-                quantize_q(1, n - 2)
-            row_shift(n)
-            if n < 6:
-                ps[n + 2, 0] = score_bank(n + 2, 0)
-            for h in range(2):
-                row_exp(n, h, ps[n, h])
+            score(n, 0)
+            score(n, 1)
+            half_max(n, 0)
+            if n > 2:
+                row_shift(n - 1)
+                row_exp(n - 1)
+            half_max(n, 1)
+        row_shift(7)
+        row_exp(7)
         g_f32 = keep.tile([P, 2, 1, 4], F32, name="g_f32")
         nc.vector.tensor_copy(out=g_f32[:, :, 0, :], in_=g_bf[:])
 
         a_shift = keep.tile([P, 8], F32, name="a_shift")
         a_raw = keep.tile([P, 8], F32, name="a_raw")
-        z = keep.tile([P, 8], F32, name="z")
         ln_z = keep.tile([P, 8], F32, name="ln_z")
         c_row = keep.tile([P, 8], F32, name="c_row")
-        b_rows = [keep.tile([P, M], F32, name="b_rows" + str(n)) for n in range(8)]
+        z = keep.tile([P, 8], F32, name="z")
+        b_rows = [keep.tile([P, 2, W], F32, name="b_rows" + str(n)) for n in range(8)]
         acc = [keep.tile([P, W], F32, name="acc" + str(h)) for h in range(2)]
 
         def b_scalar(n, h):
             nc.scalar.activation(
-                out=b_rows[n][:, W * h : W * h + W], in_=ps[n, h][:], func=ACT.Identity,
-                bias=c_row[:, n : n + 1], scale=SCALE,
+                out=b_rows[n][:, h, :], in_=ps[n][h][:], func=ACT.Identity, bias=c_row[:, n : n + 1], scale=SCALE,
             )
 
         def b_vector(n, h):
             nc.vector.tensor_scalar(
-                out=b_rows[n][:, W * h : W * h + W], in0=ps[n, h][:], scalar1=SCALE, scalar2=c_row[:, n : n + 1],
+                out=b_rows[n][:, h, :], in0=ps[n][h][:], scalar1=SCALE, scalar2=c_row[:, n : n + 1],
                 op0=ALU.mult, op1=ALU.add,
             )
 
         def col_max(n, h):
             if n == 0:
                 nc.vector.tensor_scalar(
-                    out=acc[h][:], in0=ps[n, h][:], scalar1=a_raw[:, 0:1], scalar2=None, op0=ALU.add
+                    out=acc[h][:], in0=ps[n][h][:], scalar1=a_raw[:, 0:1], scalar2=None, op0=ALU.add
                 )
             else:
                 nc.vector.scalar_tensor_tensor(
-                    out=acc[h][:], in0=ps[n, h][:], scalar=a_raw[:, n : n + 1], in1=acc[h][:], op0=ALU.add, op1=ALU.max,
+                    out=acc[h][:], in0=ps[n][h][:], scalar=a_raw[:, n : n + 1], in1=acc[h][:],
+                    op0=ALU.add, op1=ALU.max,
                 )
 
         nc.vector.tensor_tensor(out=a_shift[:], in0=a_bf[:].rearrange("p g t -> p (g t)"), in1=shift[:], op=ALU.add)
-        quantize_v(0)
         nc.vector.tensor_scalar(out=a_raw[:], in0=a_shift[:], scalar1=RAW, scalar2=None, op0=ALU.mult)
         for n in range(8):
             for h in range(2):
-                ps[n, h] = score_bank(n, h)
+                score(n, h)
             if n == 1:
                 nc.vector.tensor_tensor(out=z[:], in0=z2[:, :, 0], in1=z2[:, :, 1], op=ALU.add)
                 nc.scalar.activation(out=ln_z[:], in_=z[:], func=ACT.Ln)
+            col_max(n, 0)
             if n == 2:
                 nc.vector.tensor_tensor(out=c_row[:], in0=a_shift[:], in1=ln_z[:], op=ALU.subtract)
                 for m in range(2):
-                    b_scalar(m, 0)
-                    b_scalar(m, 1)
-            col_max(n, 0)
+                    for h in range(2):
+                        b_scalar(m, h)
             col_max(n, 1)
-            if 2 <= n < 6:
-                b_scalar(n, 0)
-                b_scalar(n, 1)
-        b_scalar(6, 0)
-        b_scalar(6, 1)
-
+            if 2 <= n < 7:
+                for h in range(2 if n < 6 else 1):
+                    b_scalar(n, h)
         h_raw = keep.tile([P, 8], F32, name="h_raw")
         h_shift = keep.tile([P, 8], F32, name="h_shift")
-        h_banks = []
-        for h in range(2):
-            xt = bank("y")
-            for c in range(4):
-                nc.tensor.transpose(xt[:, P * c : P * c + P], acc[h][:, P * c : P * c + P], ident[:])
-            h_banks.append(xt)
+        b_vector(6, 1)
         b_vector(7, 0)
         b_vector(7, 1)
+        pair = bank_pair("x")
+        for J in range(8):
+            nc.tensor.transpose(
+                pair[J // 4][:, P * (J % 4) : P * (J % 4) + P], acc[J // 4][:, P * (J % 4) : P * (J % 4) + P], ident[:]
+            )
         for h in range(2):
             nc.vector.reduce_max(
-                out=h_raw[:, 4 * h : 4 * h + 4], in_=h_banks[h][:].rearrange("p (c r) -> p c r", c=4), axis=AX.X,
+                out=h_raw[:, 4 * h : 4 * h + 4], in_=pair[h][:].rearrange("p (c r) -> p c r", c=4), axis=AX.X
             )
         nc.vector.tensor_scalar(out=h_shift[:], in0=h_raw[:], scalar1=-SCALE, scalar2=None, op0=ALU.mult)
+        quantize_v(0)
         quantize_v(2)
 
-        t_bank = {}
+        t_pair = {}
 
-        def turn_t(G, gi, u):
-            xt = bank("y")
-            for s in range(4):
-                words = t_raw[gi][:, s, :].bitcast(F32)
-                nc.tensor.transpose(xt[:, P * s : P * s + P], words[:, 256 * G + u : 256 * G + 256 : 2], ident[:])
-            t_bank[G, gi, u] = xt
+        def turn_t(G, gi):
+            t_pair[G, gi] = bank_pair("y")
+            for u in range(2):
+                for s in range(4):
+                    words = t_raw[gi][:, s, :].bitcast(F32)
+                    nc.tensor.transpose(
+                        t_pair[G, gi][u][:, P * s : P * s + P], words[:, 256 * G + u : 256 * G + 256 : 2], ident[:]
+                    )
 
         e_cols = {}
         ez = keep.tile([P, 8, 2], F32, name="ez")
@@ -278,20 +283,18 @@ def tile_sinkhorninverseotresidualpull_x1_kernel(tc, q, k, a, t, g, v, out_0, ou
         w_col = keep.tile([P, 8], F32, name="w_col")
 
         def col_exp(J):
-            e = work.tile([P, N], F32, name="e_cols", tag="e_cols", bufs=8)
-            e_cols[J] = e
-            banks = []
+            e_cols[J] = work.tile([P, 2, W], F32, name="e_cols", tag="e_cols", bufs=8)
+            pair = bank_pair("x")
             for gi in range(2):
-                xt = bank("x")
                 for s in range(4):
                     nc.tensor.transpose(
-                        xt[:, P * s : P * s + P], b_rows[4 * gi + s][:, P * J : P * J + P], ident[:]
+                        pair[gi][:, P * s : P * s + P],
+                        b_rows[4 * gi + s][:, J // 4, P * (J % 4) : P * (J % 4) + P], ident[:]
                     )
-                banks.append(xt)
             for gi in range(2):
                 nc.scalar.activation(
-                    out=e[:, W * gi : W * gi + W], in_=banks[gi][:], func=ACT.Exp,
-                    bias=h_shift[:, J : J + 1], accum_out=ez[:, J, gi : gi + 1],
+                    out=e_cols[J][:, gi, :], in_=pair[gi][:], func=ACT.Exp, bias=h_shift[:, J : J + 1],
+                    accum_out=ez[:, J, gi : gi + 1],
                 )
 
         def col_sum(J):
@@ -305,15 +308,16 @@ def tile_sinkhorninverseotresidualpull_x1_kernel(tc, q, k, a, t, g, v, out_0, ou
 
         residual = {}
         r_quads = {}
+        gained = {}
 
         def col_residual(J, gi):
             G, s = divmod(J, 4)
             if s == 0:
                 residual[G, gi] = work.tile([P, 4, W], F32, name="residual", tag="wide", bufs=4)
             u, e = divmod(s, 2)
-            t_view = t_bank[G, gi, u][:].bitcast(BF16).rearrange("p (i e) -> p i e", e=2)[:, :, e]
+            t_view = t_pair[G, gi][u][:].bitcast(BF16).rearrange("p (i e) -> p i e", e=2)[:, :, e]
             nc.vector.scalar_tensor_tensor(
-                out=residual[G, gi][:, s, :], in0=e_cols[J][:, W * gi : W * gi + W], scalar=w_col[:, J : J + 1],
+                out=residual[G, gi][:, s, :], in0=e_cols[J][:, gi, :], scalar=w_col[:, J : J + 1],
                 in1=t_view, op0=ALU.mult, op1=ALU.subtract,
             )
 
@@ -327,32 +331,27 @@ def tile_sinkhorninverseotresidualpull_x1_kernel(tc, q, k, a, t, g, v, out_0, ou
                 in1=g_f32[:, G, :, :].to_broadcast([P, hi - lo, 4]), op=ALU.mult,
             )
 
-        gained = {}
-
-        def gain_scalar(J, gi, lo, hi):
+        def gain_scalar(J, gi):
             G, s = divmod(J, 4)
             if s == 0:
                 gained[G, gi] = work.tile([P, 4, W], BF16, name="gained", tag="gained", bufs=2)
             nc.scalar.activation(
-                out=gained[G, gi][:, s, lo:hi], in_=residual[G, gi][:, s, lo:hi], func=ACT.Copy,
+                out=gained[G, gi][:, s, :], in_=residual[G, gi][:, s, :], func=ACT.Copy,
                 scale=g_f32[:, G, 0, s : s + 1],
             )
 
-        def gain_gather(G, gi, lo, hi):
-            nc.vector.tensor_copy(
-                out=r_quads[G, gi][:, lo:hi, :], in_=gained[G, gi][:].rearrange("p t i -> p i t")[:, lo:hi, :]
-            )
+        def gain_gather(G, gi):
+            new_quads(G, gi)
+            nc.vector.tensor_copy(out=r_quads[G, gi][:], in_=gained[G, gi][:].rearrange("p t i -> p i t"))
 
         def quantize_r(G, gi):
             quantize(r_quads[G, gi][:], r_codes[G], r_scales[G], slice(W * gi, W * gi + W))
 
-        turn_t(0, 0, 0)
+        turn_t(0, 0)
         col_exp(0)
-        turn_t(0, 0, 1)
         col_exp(1)
-        turn_t(1, 0, 0)
-        turn_t(1, 0, 1)
-        FILL = {3: 0, 4: 1, 5: 2}
+        turn_t(1, 0)
+        FILL = {4: 0, 5: 1, 6: 2}
         for J in range(8):
             col_sum(J)
             if J in FILL:
@@ -361,29 +360,24 @@ def tile_sinkhorninverseotresidualpull_x1_kernel(tc, q, k, a, t, g, v, out_0, ou
             col_residual(J, 0)
             if J < 6:
                 col_exp(J + 2)
-            if J == 1:
-                turn_t(0, 1, 0)
             if J == 3:
+                turn_t(0, 1)
                 new_quads(0, 0)
-                for lo in range(0, W, 128):
-                    gain_pool(0, 0, lo, lo + 128)
-            if J == 4:
-                turn_t(0, 1, 1)
-        turn_t(1, 1, 0)
-        turn_t(1, 1, 1)
+                for lo in range(0, W, 64):
+                    gain_pool(0, 0, lo, lo + 64)
+        turn_t(1, 1)
         for J in range(4, 8):
-            gain_scalar(J, 0, 0, 384)
-        new_quads(1, 0)
-        gain_pool(1, 0, 384, W)
+            gain_scalar(J, 0)
         quantize_r(0, 0)
         col_residual(3, 1)
-        gain_gather(1, 0, 0, 384)
-        new_quads(0, 1)
-        for lo in range(0, W, 128):
-            gain_pool(0, 1, lo, lo + 128)
+        gain_gather(1, 0)
+        for J in range(4):
+            gain_scalar(J, 1)
+        col_residual(4, 1)
         quantize_r(1, 0)
-        for J in range(4, 8):
+        for J in range(5, 8):
             col_residual(J, 1)
+        gain_gather(0, 1)
 
         out_wide = {}
         out_quads = {}
@@ -414,10 +408,7 @@ def tile_sinkhorninverseotresidualpull_x1_kernel(tc, q, k, a, t, g, v, out_0, ou
                 )
 
         def s_out(dst, src):
-            nc.scalar.activation(out=dst, in_=src, func=ACT.Copy, scale=1.0 / math.sqrt(M))
-
-        def v_out(dst, src):
-            nc.vector.tensor_scalar(out=dst, in0=src, scalar1=1.0 / math.sqrt(M), scalar2=None, op0=ALU.mult)
+            nc.scalar.activation(out=dst, in_=src, func=ACT.Copy, scale=PULL)
 
         def out_gather(gi, f0, fw):
             quads = work.tile([P, fw, 4], BF16, name="out_quads", tag="quads", bufs=4, align_bytes=64)
@@ -443,19 +434,13 @@ def tile_sinkhorninverseotresidualpull_x1_kernel(tc, q, k, a, t, g, v, out_0, ou
                         in_=out_scales[gi][32 * Q : 32 * Q + 4, :].bitcast(I32),
                     )
 
-        gain_scalar(4, 1, 0, 256)
-        gain_scalar(5, 1, 0, 256)
         for s in range(4):
             pull_bank(0, 0, W, s, "x", s_out)
-            if s < 2:
-                gain_scalar(6 + s, 1, 0, 256)
+            gain_scalar(4 + s, 1)
         quantize_v(1)
         quantize_v(3)
-        new_quads(1, 1)
-        gain_pool(1, 1, 256, 384)
-        gain_pool(1, 1, 384, W)
-        gain_gather(1, 1, 0, 256)
         quantize_r(0, 1)
+        gain_gather(1, 1)
         for s in range(4):
             pull_bank(0, W, W, s, "x", s_out)
         out_gather(0, 0, W)

@@ -56,6 +56,9 @@ def tile_sinkhorninverseotresidualpull_x1_kernel(tc, q, k, a, t, g, v, out_0, ou
         nc.vector.memset(warm[:], 0.0)
         nc.scalar.activation(out=warm[:, 1:2], in_=warm[:, 0:1], func=ACT.Exp)
 
+        zeros = keep.tile([P, W], BF16, name="zeros")
+        nc.vector.memset(zeros[:], 0.0)
+
         k_codes = keep.tile([P, M], U32, name="k_codes", align_bytes=64)
         k_scales = keep.tile([P, M], U8, name="k_scales", align_bytes=64)
         q_codes = keep.tile([P, N], U32, name="q_codes", align_bytes=64)
@@ -70,6 +73,15 @@ def tile_sinkhorninverseotresidualpull_x1_kernel(tc, q, k, a, t, g, v, out_0, ou
 
         def bank_pair(tag):
             return [bank(tag), bank(tag)]
+
+        def warm_plain(b):
+            nc.tensor.matmul(b[:], lhsT=zeros[:, 0:P], rhs=zeros[:], start=True, stop=True)
+
+        def warm_mx(b):
+            nc.tensor.matmul_mx(
+                out=b[:], lhsT=k_codes[:, 0:P].bitcast(FP8X4), lhsT_scale=k_scales[:, 0:P],
+                rhs=k_codes[:, 0:W].bitcast(FP8X4), rhs_scale=k_scales[:, 0:W], start=True, stop=True,
+            )
 
         def quad_tile(name):
             return work.tile([P, W, 4], BF16, name=name, tag="quads", bufs=4, align_bytes=64)
@@ -159,12 +171,17 @@ def tile_sinkhorninverseotresidualpull_x1_kernel(tc, q, k, a, t, g, v, out_0, ou
         pq0 = bank_pair("y")
         pk1 = bank_pair("x")
         pq1 = bank_pair("y")
+        for b in (pk0[0], pk0[1], pq0[0], pq0[1]):
+            warm_plain(b)
         turn_rows(k_raw[0], kq[0], pk0, 0, s_copy)
+        warm_plain(pk1[0])
         turn_rows(k_raw[0], kq[0], pk0, 1, v_copy)
         turn_rows(q_raw[0], qq[0], pq0, 0, s_copy)
+        warm_plain(pk1[1])
         quantize_k(0)
         quantize_q(0, 0)
         turn_rows(q_raw[0], qq[0], pq0, 1, s_copy)
+        warm_plain(pq1[0])
         turn_rows(k_raw[1], kq[1], pk1, 0, s_copy)
         score(0, 0)
         score(1, 0)
@@ -254,6 +271,8 @@ def tile_sinkhorninverseotresidualpull_x1_kernel(tc, q, k, a, t, g, v, out_0, ou
         b_vector(7, 0)
         b_vector(7, 1)
         pair = bank_pair("x")
+        warm_mx(pair[0])
+        warm_mx(pair[1])
         for J in range(8):
             nc.tensor.transpose(
                 pair[J // 4][:, P * (J % 4) : P * (J % 4) + P], acc[J // 4][:, P * (J % 4) : P * (J % 4) + P], ident[:]
@@ -268,14 +287,12 @@ def tile_sinkhorninverseotresidualpull_x1_kernel(tc, q, k, a, t, g, v, out_0, ou
 
         t_pair = {}
 
-        def turn_t(G, gi):
-            t_pair[G, gi] = bank_pair("y")
-            for u in range(2):
-                for s in range(4):
-                    words = t_raw[gi][:, s, :].bitcast(F32)
-                    nc.tensor.transpose(
-                        t_pair[G, gi][u][:, P * s : P * s + P], words[:, 256 * G + u : 256 * G + 256 : 2], ident[:]
-                    )
+        def turn_t(G, gi, u):
+            xt = bank("y")
+            t_pair[G, gi, u] = xt
+            for s in range(4):
+                words = t_raw[gi][:, s, :].bitcast(F32)
+                nc.tensor.transpose(xt[:, P * s : P * s + P], words[:, 256 * G + u : 256 * G + 256 : 2], ident[:])
 
         e_cols = {}
         ez = keep.tile([P, 8, 2], F32, name="ez")
@@ -286,6 +303,8 @@ def tile_sinkhorninverseotresidualpull_x1_kernel(tc, q, k, a, t, g, v, out_0, ou
             e_cols[J] = work.tile([P, 2, W], F32, name="e_cols", tag="e_cols", bufs=8)
             pair = bank_pair("x")
             for gi in range(2):
+                if gi == 0 or J % 2 == 0:
+                    warm_mx(pair[gi])
                 for s in range(4):
                     nc.tensor.transpose(
                         pair[gi][:, P * s : P * s + P],
@@ -315,7 +334,7 @@ def tile_sinkhorninverseotresidualpull_x1_kernel(tc, q, k, a, t, g, v, out_0, ou
             if s == 0:
                 residual[G, gi] = work.tile([P, 4, W], F32, name="residual", tag="wide", bufs=4)
             u, e = divmod(s, 2)
-            t_view = t_pair[G, gi][u][:].bitcast(BF16).rearrange("p (i e) -> p i e", e=2)[:, :, e]
+            t_view = t_pair[G, gi, u][:].bitcast(BF16).rearrange("p (i e) -> p i e", e=2)[:, :, e]
             nc.vector.scalar_tensor_tensor(
                 out=residual[G, gi][:, s, :], in0=e_cols[J][:, gi, :], scalar=w_col[:, J : J + 1],
                 in1=t_view, op0=ALU.mult, op1=ALU.subtract,
@@ -347,10 +366,10 @@ def tile_sinkhorninverseotresidualpull_x1_kernel(tc, q, k, a, t, g, v, out_0, ou
         def quantize_r(G, gi):
             quantize(r_quads[G, gi][:], r_codes[G], r_scales[G], slice(W * gi, W * gi + W))
 
-        turn_t(0, 0)
+        turn_t(0, 0, 0)
+        turn_t(0, 0, 1)
         col_exp(0)
         col_exp(1)
-        turn_t(1, 0)
         FILL = {4: 0, 5: 1, 6: 2}
         for J in range(8):
             col_sum(J)
@@ -360,52 +379,57 @@ def tile_sinkhorninverseotresidualpull_x1_kernel(tc, q, k, a, t, g, v, out_0, ou
             col_residual(J, 0)
             if J < 6:
                 col_exp(J + 2)
+            if J in (0, 1):
+                turn_t(1, 0, J)
+            if J in (2, 4):
+                turn_t(0, 1, J // 2 - 1)
             if J == 3:
-                turn_t(0, 1)
                 new_quads(0, 0)
                 for lo in range(0, W, 64):
                     gain_pool(0, 0, lo, lo + 64)
-        turn_t(1, 1)
-        for J in range(4, 8):
-            gain_scalar(J, 0)
-        quantize_r(0, 0)
-        col_residual(3, 1)
-        gain_gather(1, 0)
-        for J in range(4):
-            gain_scalar(J, 1)
-        col_residual(4, 1)
-        quantize_r(1, 0)
-        for J in range(5, 8):
-            col_residual(J, 1)
-        gain_gather(0, 1)
-
         out_wide = {}
         out_quads = {}
         out_scales = {}
 
-        def pull_bank(gi, f0, fw, s0, tag, copy):
-            step = W // fw
+        out_banks = {}
+
+        def pull_open(gi, f0, s, tag):
+            out_banks[gi, f0, s] = bank(tag)
+            pull_pass(gi, f0, W, s, 0, out_banks[gi, f0, s][:])
+
+        def pull_pass(gi, f0, fw, s, G, dst):
+            cols = slice(W * gi + P * s, W * gi + P * s + P)
             f_cols = slice(f0, f0 + fw)
-            if s0 == 0:
-                out_wide[gi, f0] = work.tile([P, 4, fw], F32, name="out_wide", tag="wide", bufs=4)
-            wide = out_wide[gi, f0]
-            ps = bank(tag)
-            for s in range(s0, s0 + step):
-                cols = slice(W * gi + P * s, W * gi + P * s + P)
+            nc.tensor.matmul_mx(
+                out=dst,
+                lhsT=r_codes[G][:, cols].bitcast(FP8X4), lhsT_scale=r_scales[G][:, cols],
+                rhs=v_codes[G][:, f_cols].bitcast(FP8X4), rhs_scale=v_scales[G][:, f_cols],
+                start=(G == 0), stop=(G == 1),
+            )
+
+        def store_rows(gi, f0, fw, s):
+            nc.sync.dma_start(
+                out=out_0[W * gi : W * gi + W, :].rearrange("(p t) f -> p t f", t=4)[:, s : s + 2, f0 : f0 + fw],
+                in_=out_wide[gi, f0][:, s : s + 2, :],
+            )
+
+        def pull_close(gi, f0, s, copy):
+            if s == 0:
+                out_wide[gi, f0] = work.tile([P, 4, W], F32, name="out_wide", tag="wide", bufs=4)
+            pull_pass(gi, f0, W, s, 1, out_banks[gi, f0, s][:])
+            copy(out_wide[gi, f0][:, s, :], out_banks[gi, f0, s][:])
+            if s % 2 == 1:
+                store_rows(gi, f0, W, s - 1)
+
+        def pull_quarter(gi, f0, s, tag, copy):
+            if s == 0:
+                out_wide[gi, f0] = work.tile([P, 4, 256], F32, name="out_wide", tag="wide", bufs=4)
+            xt = bank(tag)
+            for c in range(2):
                 for G in range(2):
-                    nc.tensor.matmul_mx(
-                        out=ps[:, fw * (s - s0) : fw * (s - s0) + fw],
-                        lhsT=r_codes[G][:, cols].bitcast(FP8X4), lhsT_scale=r_scales[G][:, cols],
-                        rhs=v_codes[G][:, f_cols].bitcast(FP8X4), rhs_scale=v_scales[G][:, f_cols],
-                        start=(G == 0), stop=(G == 1),
-                    )
-            copy(wide[:, s0 : s0 + step, :], ps[:].rearrange("p (t f) -> p t f", t=step))
-            if (s0 + step) % 2 == 0:
-                s_lo = s0 + step - 2
-                nc.sync.dma_start(
-                    out=out_0[W * gi : W * gi + W, :].rearrange("(p t) f -> p t f", t=4)[:, s_lo : s_lo + 2, f_cols],
-                    in_=wide[:, s_lo : s_lo + 2, :],
-                )
+                    pull_pass(gi, f0, 256, s + c, G, xt[:, 256 * c : 256 * c + 256])
+            copy(out_wide[gi, f0][:, s : s + 2, :], xt[:].rearrange("p (t f) -> p t f", t=2))
+            store_rows(gi, f0, 256, s)
 
         def s_out(dst, src):
             nc.scalar.activation(out=dst, in_=src, func=ACT.Copy, scale=PULL)
@@ -434,24 +458,45 @@ def tile_sinkhorninverseotresidualpull_x1_kernel(tc, q, k, a, t, g, v, out_0, ou
                         in_=out_scales[gi][32 * Q : 32 * Q + 4, :].bitcast(I32),
                     )
 
+        for u in range(2):
+            turn_t(1, 1, u)
+        for J in range(4, 8):
+            gain_scalar(J, 0)
+        quantize_r(0, 0)
         for s in range(4):
-            pull_bank(0, 0, W, s, "x", s_out)
+            pull_open(0, 0, s, "x")
+        col_residual(3, 1)
+        gain_gather(1, 0)
+        for J in range(4):
+            gain_scalar(J, 1)
+        col_residual(4, 1)
+        quantize_r(1, 0)
+        for J in range(5, 8):
+            col_residual(J, 1)
+        gain_gather(0, 1)
+
+        for s in range(4):
+            pull_close(0, 0, s, s_out)
             gain_scalar(4 + s, 1)
         quantize_v(1)
         quantize_v(3)
+        for s in range(4):
+            pull_open(0, W, s, "x")
         quantize_r(0, 1)
         gain_gather(1, 1)
         for s in range(4):
-            pull_bank(0, W, W, s, "x", s_out)
+            pull_close(0, W, s, s_out)
+        for s in range(4):
+            pull_open(1, 0, s, "y")
         out_gather(0, 0, W)
         quantize_r(1, 1)
         out_quantize(0, 0, W)
         for s in range(4):
-            pull_bank(1, 0, W, s, "y", s_out)
+            pull_close(1, 0, s, s_out)
         out_gather(0, W, W)
         for f0 in (W, 768):
-            for s0 in (0, 2):
-                pull_bank(1, f0, 256, s0, "x", s_out)
+            for s in (0, 2):
+                pull_quarter(1, f0, s, "x", s_out)
         out_quantize(0, W, W)
         out_gather(1, 0, W)
         out_gather(1, W, 256)

@@ -32,32 +32,35 @@ def tile_sinkhorninverseotresidualpull_x1_kernel(tc, q, k, a, t, g, v, out_0, ou
         psum = ctx.enter_context(tc.psum_pool(name="psum", bufs=4))
         ctx.enter_context(tc.manual_schedule())
 
-        k_raw, q_raw, v_raw, t_raw = [], [], [], []
-        for G in range(2):
-            for dst, src, name in ((k_raw, k, "k_raw"), (q_raw, q, "q_raw")):
-                raw = keep.tile([P, 4, D], BF16, name=name + str(G))
-                rows = src[W * G : W * G + W, :].rearrange("(p t) d -> p t d", t=4)
-                for c in range(2):
-                    nc.sync.dma_start(out=raw[:, 2 * c : 2 * c + 2, :], in_=rows[:, 2 * c : 2 * c + 2, :])
-                dst.append(raw)
+        k_raw = [keep.tile([P, 4, D], BF16, name="k_raw" + str(G)) for G in range(2)]
+        q_raw = [keep.tile([P, 4, D], BF16, name="q_raw" + str(G)) for G in range(2)]
+        v_raw = [keep.tile([P, 4, F], BF16, name="v_raw" + str(G)) for G in range(2)]
+        t_raw = [keep.tile([P, 4, M], BF16, name="t_raw" + str(G)) for G in range(2)]
+
+        def load_half(dst, src, G, c):
+            rows = src[W * G : W * G + W, :].rearrange("(p t) d -> p t d", t=4)
+            nc.sync.dma_start(out=dst[G][:, 2 * c : 2 * c + 2, :], in_=rows[:, 2 * c : 2 * c + 2, :])
+
+        for dst, src, G, c in (
+            (k_raw, k, 0, 0), (k_raw, k, 0, 1), (q_raw, q, 0, 0), (k_raw, k, 1, 0),
+            (k_raw, k, 1, 1), (q_raw, q, 0, 1), (q_raw, q, 1, 0), (q_raw, q, 1, 1),
+        ):
+            load_half(dst, src, G, c)
         a_bf = keep.tile([P, 2, 4], BF16, name="a_bf")
         g_bf = keep.tile([P, 2, 4], BF16, name="g_bf")
         nc.sync.dma_start(out=a_bf[:], in_=a.rearrange("(g p t) -> p g t", g=2, t=4))
         nc.sync.dma_start(out=g_bf[:], in_=g.rearrange("(g p t) -> p g t", g=2, t=4))
-        for dst, src, name in ((v_raw, v, "v_raw"), (t_raw, t, "t_raw")):
+        for dst, src in ((v_raw, v), (t_raw, t)):
             for G in range(2):
-                raw = keep.tile([P, 4, 1024], BF16, name=name + str(G))
-                nc.sync.dma_start(out=raw[:], in_=src[W * G : W * G + W, :].rearrange("(p t) d -> p t d", t=4))
-                dst.append(raw)
+                nc.sync.dma_start(out=dst[G][:], in_=src[W * G : W * G + W, :].rearrange("(p t) d -> p t d", t=4))
 
+        zeros = keep.tile([P, P], F32, name="zeros")
+        nc.vector.memset(zeros[:], 0.0)
         ident = keep.tile([P, P], F32, name="ident")
         make_identity(nc, ident[:])
         warm = keep.tile([P, 2], F32, name="warm")
         nc.vector.memset(warm[:], 0.0)
         nc.scalar.activation(out=warm[:, 1:2], in_=warm[:, 0:1], func=ACT.Exp)
-
-        zeros = keep.tile([P, W], BF16, name="zeros")
-        nc.vector.memset(zeros[:], 0.0)
 
         k_codes = keep.tile([P, M], U32, name="k_codes", align_bytes=64)
         k_scales = keep.tile([P, M], U8, name="k_scales", align_bytes=64)
@@ -74,14 +77,8 @@ def tile_sinkhorninverseotresidualpull_x1_kernel(tc, q, k, a, t, g, v, out_0, ou
         def bank_pair(tag):
             return [bank(tag), bank(tag)]
 
-        def warm_plain(b):
-            nc.tensor.matmul(b[:], lhsT=zeros[:, 0:P], rhs=zeros[:], start=True, stop=True)
-
-        def warm_mx(b):
-            nc.tensor.matmul_mx(
-                out=b[:], lhsT=k_codes[:, 0:P].bitcast(FP8X4), lhsT_scale=k_scales[:, 0:P],
-                rhs=k_codes[:, 0:W].bitcast(FP8X4), rhs_scale=k_scales[:, 0:W], start=True, stop=True,
-            )
+        def keep_clock(b):
+            nc.tensor.matmul(b[:, 0:P], lhsT=zeros[:], rhs=zeros[:], start=True, stop=True)
 
         def quad_tile(name):
             return work.tile([P, W, 4], BF16, name=name, tag="quads", bufs=4, align_bytes=64)
@@ -93,9 +90,9 @@ def tile_sinkhorninverseotresidualpull_x1_kernel(tc, q, k, a, t, g, v, out_0, ou
                 in_=quads.rearrange("p c t -> p (c t)"),
             )
 
-        def turn_rows(raw, quads, pair, c, copy):
+        def turn_rows(raw, quads, b, c, copy):
             words = raw[:].bitcast(F32)
-            xt = pair[c][:].rearrange("p (s u r) -> p s u r", s=2, u=2)
+            xt = b[:].rearrange("p (s u r) -> p s u r", s=2, u=2)
             for s in range(2):
                 for u in range(2):
                     nc.tensor.transpose(xt[:, s, u, :], words[:, 2 * c + s, u : D // 2 : 2], ident[:])
@@ -140,15 +137,16 @@ def tile_sinkhorninverseotresidualpull_x1_kernel(tc, q, k, a, t, g, v, out_0, ou
         z2 = keep.tile([P, 8, 2], F32, name="z2")
         ps = {}
 
-        def score(n, h):
+        def score(n, h, times=1):
             if h == 0:
-                ps[n] = bank_pair(TAGS[n % 2])
-            nc.tensor.matmul_mx(
-                out=ps[n][h][:],
-                lhsT=q_codes[:, P * n : P * n + P].bitcast(FP8X4), lhsT_scale=q_scales[:, P * n : P * n + P],
-                rhs=k_codes[:, W * h : W * h + W].bitcast(FP8X4), rhs_scale=k_scales[:, W * h : W * h + W],
-                start=True, stop=True,
-            )
+                ps[n] = bank_pair(TAGS[n // 2 % 2])
+            for i in range(times):
+                nc.tensor.matmul_mx(
+                    out=ps[n][h][:],
+                    lhsT=q_codes[:, P * n : P * n + P].bitcast(FP8X4), lhsT_scale=q_scales[:, P * n : P * n + P],
+                    rhs=k_codes[:, W * h : W * h + W].bitcast(FP8X4), rhs_scale=k_scales[:, W * h : W * h + W],
+                    start=True, stop=True,
+                )
 
         def half_max(n, h):
             nc.vector.reduce_max(out=maxes[:, n, h : h + 1], in_=ps[n][h][:], axis=AX.X)
@@ -167,51 +165,57 @@ def tile_sinkhorninverseotresidualpull_x1_kernel(tc, q, k, a, t, g, v, out_0, ou
                     accum_out=z2[:, n, h : h + 1],
                 )
 
-        pk0 = bank_pair("x")
-        pq0 = bank_pair("y")
-        pk1 = bank_pair("x")
-        pq1 = bank_pair("y")
-        for b in (pk0[0], pk0[1], pq0[0], pq0[1]):
-            warm_plain(b)
-        turn_rows(k_raw[0], kq[0], pk0, 0, s_copy)
-        warm_plain(pk1[0])
-        turn_rows(k_raw[0], kq[0], pk0, 1, v_copy)
-        turn_rows(q_raw[0], qq[0], pq0, 0, s_copy)
-        warm_plain(pk1[1])
+        turned = {}
+        for name, tag in (("k0", "x"), ("k1", "x"), ("q0", "y"), ("q1", "y")):
+            for c in range(2):
+                turned[name, c] = bank(tag)
+        for b in (("k0", 0), ("k0", 1), ("k1", 0), ("k1", 1), ("q0", 0)):
+            keep_clock(turned[b])
+        turn_rows(k_raw[0], kq[0], turned["k0", 0], 0, s_copy)
+        keep_clock(turned["q0", 1])
+        turn_rows(k_raw[0], kq[0], turned["k0", 1], 1, v_copy)
+        keep_clock(turned["q1", 0])
+        turn_rows(q_raw[0], qq[0], turned["q0", 0], 0, s_copy)
+        keep_clock(turned["q1", 1])
         quantize_k(0)
         quantize_q(0, 0)
-        turn_rows(q_raw[0], qq[0], pq0, 1, s_copy)
-        warm_plain(pq1[0])
-        turn_rows(k_raw[1], kq[1], pk1, 0, s_copy)
-        score(0, 0)
-        score(1, 0)
-        half_max(0, 0)
-        quantize_q(0, 1)
-        half_max(1, 0)
-        turn_rows(k_raw[1], kq[1], pk1, 1, s_copy)
-        turn_rows(q_raw[1], qq[1], pq1, 0, s_copy)
+        turn_rows(k_raw[1], kq[1], turned["k1", 0], 0, s_copy)
+        keep_clock(turned["q1", 1])
+        turn_rows(k_raw[1], kq[1], turned["k1", 1], 1, v_copy)
         quantize_k(1)
-        turn_rows(q_raw[1], qq[1], pq1, 1, s_copy)
-        for n in range(2):
-            score(n, 1)
+        keep_clock(turned["q1", 1])
+        turn_rows(q_raw[0], qq[0], turned["q0", 1], 1, s_copy)
+        score(0, 0)
+        half_max(0, 0)
+        turn_rows(q_raw[1], qq[1], turned["q1", 0], 0, s_copy)
+        score(0, 1)
+        score(1, 0)
+        score(1, 1)
         half_max(0, 1)
         row_shift(0)
-        half_max(1, 1)
+        quantize_q(0, 1)
+        turn_rows(q_raw[1], qq[1], turned["q1", 1], 1, s_copy)
         row_exp(0)
-        quantize_q(1, 0)
+        half_max(1, 0)
+        half_max(1, 1)
         row_shift(1)
         row_exp(1)
-        quantize_q(1, 1)
-        for i in range(4):
-            gather_v(i)
         for n in range(2, 8):
             score(n, 0)
             score(n, 1)
             half_max(n, 0)
-            if n > 2:
+            if n > 3:
                 row_shift(n - 1)
                 row_exp(n - 1)
             half_max(n, 1)
+            if n == 2:
+                row_shift(n)
+                row_exp(n)
+                quantize_q(1, 0)
+            if n == 3:
+                quantize_q(1, 1)
+                for i in range(4):
+                    gather_v(i)
         row_shift(7)
         row_exp(7)
         g_f32 = keep.tile([P, 2, 1, 4], F32, name="g_f32")
@@ -251,7 +255,7 @@ def tile_sinkhorninverseotresidualpull_x1_kernel(tc, q, k, a, t, g, v, out_0, ou
         nc.vector.tensor_scalar(out=a_raw[:], in0=a_shift[:], scalar1=RAW, scalar2=None, op0=ALU.mult)
         for n in range(8):
             for h in range(2):
-                score(n, h)
+                score(n, h, 2 if n > 5 else 1)
             if n == 1:
                 nc.vector.tensor_tensor(out=z[:], in0=z2[:, :, 0], in1=z2[:, :, 1], op=ALU.add)
                 nc.scalar.activation(out=ln_z[:], in_=z[:], func=ACT.Ln)
@@ -271,8 +275,8 @@ def tile_sinkhorninverseotresidualpull_x1_kernel(tc, q, k, a, t, g, v, out_0, ou
         b_vector(7, 0)
         b_vector(7, 1)
         pair = bank_pair("x")
-        warm_mx(pair[0])
-        warm_mx(pair[1])
+        keep_clock(pair[0])
+        keep_clock(pair[0])
         for J in range(8):
             nc.tensor.transpose(
                 pair[J // 4][:, P * (J % 4) : P * (J % 4) + P], acc[J // 4][:, P * (J % 4) : P * (J % 4) + P], ident[:]
@@ -287,9 +291,11 @@ def tile_sinkhorninverseotresidualpull_x1_kernel(tc, q, k, a, t, g, v, out_0, ou
 
         t_pair = {}
 
-        def turn_t(G, gi, u):
+        def turn_t(G, gi, u, clock=0):
             xt = bank("y")
             t_pair[G, gi, u] = xt
+            for i in range(clock):
+                keep_clock(xt)
             for s in range(4):
                 words = t_raw[gi][:, s, :].bitcast(F32)
                 nc.tensor.transpose(xt[:, P * s : P * s + P], words[:, 256 * G + u : 256 * G + 256 : 2], ident[:])
@@ -299,27 +305,38 @@ def tile_sinkhorninverseotresidualpull_x1_kernel(tc, q, k, a, t, g, v, out_0, ou
         ezs = keep.tile([P, 8], F32, name="ezs")
         w_col = keep.tile([P, 8], F32, name="w_col")
 
-        def col_exp(J):
+        e_pair = {}
+
+        def turn_b(J):
             e_cols[J] = work.tile([P, 2, W], F32, name="e_cols", tag="e_cols", bufs=8)
             pair = bank_pair("x")
             for gi in range(2):
                 if gi == 0 or J % 2 == 0:
-                    warm_mx(pair[gi])
+                    keep_clock(pair[gi])
                 for s in range(4):
                     nc.tensor.transpose(
                         pair[gi][:, P * s : P * s + P],
                         b_rows[4 * gi + s][:, J // 4, P * (J % 4) : P * (J % 4) + P], ident[:]
                     )
-            for gi in range(2):
+            e_pair[J] = pair
+
+        def col_exp(J, halves=(0, 1)):
+            for gi in halves:
                 nc.scalar.activation(
-                    out=e_cols[J][:, gi, :], in_=pair[gi][:], func=ACT.Exp, bias=h_shift[:, J : J + 1],
+                    out=e_cols[J][:, gi, :], in_=e_pair[J][gi][:], func=ACT.Exp, bias=h_shift[:, J : J + 1],
                     accum_out=ez[:, J, gi : gi + 1],
                 )
 
         def col_sum(J):
-            nc.vector.tensor_scalar(
-                out=ezs[:, J : J + 1], in0=ez[:, J, 0:1], scalar1=ez[:, J, 1:2], scalar2=1.0 / M,
-                op0=ALU.add, op1=ALU.mult,
+            if J not in S_SUM:
+                nc.vector.tensor_scalar(
+                    out=ezs[:, J : J + 1], in0=ez[:, J, 0:1], scalar1=ez[:, J, 1:2], scalar2=1.0 / M,
+                    op0=ALU.add, op1=ALU.mult,
+                )
+                return
+            both = keep.tile([P, 2], F32, name="both" + str(J))
+            nc.scalar.activation(
+                out=both[:], in_=ez[:, J, :], func=ACT.Copy, scale=1.0 / M, accum_out=ezs[:, J : J + 1],
             )
 
         def col_weight(J):
@@ -359,42 +376,56 @@ def tile_sinkhorninverseotresidualpull_x1_kernel(tc, q, k, a, t, g, v, out_0, ou
                 scale=g_f32[:, G, 0, s : s + 1],
             )
 
-        def gain_gather(G, gi):
-            new_quads(G, gi)
-            nc.vector.tensor_copy(out=r_quads[G, gi][:], in_=gained[G, gi][:].rearrange("p t i -> p i t"))
+        def gain_gather(G, gi, lo, hi):
+            if lo == 0:
+                new_quads(G, gi)
+            nc.vector.tensor_copy(
+                out=r_quads[G, gi][:, lo:hi, :], in_=gained[G, gi][:].rearrange("p t i -> p i t")[:, lo:hi, :]
+            )
 
-        def quantize_r(G, gi):
-            quantize(r_quads[G, gi][:], r_codes[G], r_scales[G], slice(W * gi, W * gi + W))
+        def quantize_r(G, gi, lo=0, hi=W):
+            quantize(r_quads[G, gi][:, lo:hi, :], r_codes[G], r_scales[G], slice(W * gi + lo, W * gi + hi))
 
+        turn_b(0)
         turn_t(0, 0, 0)
+        turn_b(1)
         turn_t(0, 0, 1)
         col_exp(0)
-        col_exp(1)
         FILL = {4: 0, 5: 1, 6: 2}
+        S_SUM = (4, 5, 6)
         for J in range(8):
+            if J < 7:
+                col_exp(J + 1, (0,))
             col_sum(J)
-            if J in FILL:
-                col_residual(FILL[J], 1)
-            col_weight(J)
-            col_residual(J, 0)
+            if J < 7:
+                col_exp(J + 1, (1,))
             if J < 6:
-                col_exp(J + 2)
+                turn_b(J + 2)
             if J in (0, 1):
                 turn_t(1, 0, J)
             if J in (2, 4):
                 turn_t(0, 1, J // 2 - 1)
+            col_weight(J)
+            if J in FILL:
+                col_residual(FILL[J], 1)
+            if J in (1, 2):
+                quantize_v(2 * J - 1)
+            col_residual(J, 0)
             if J == 3:
                 new_quads(0, 0)
                 for lo in range(0, W, 64):
                     gain_pool(0, 0, lo, lo + 64)
+
         out_wide = {}
         out_quads = {}
         out_scales = {}
 
         out_banks = {}
 
-        def pull_open(gi, f0, s, tag):
+        def pull_bank(gi, f0, s, tag):
             out_banks[gi, f0, s] = bank(tag)
+
+        def pull_open(gi, f0, s):
             pull_pass(gi, f0, W, s, 0, out_banks[gi, f0, s][:])
 
         def pull_pass(gi, f0, fw, s, G, dst):
@@ -434,10 +465,13 @@ def tile_sinkhorninverseotresidualpull_x1_kernel(tc, q, k, a, t, g, v, out_0, ou
         def s_out(dst, src):
             nc.scalar.activation(out=dst, in_=src, func=ACT.Copy, scale=PULL)
 
-        def out_gather(gi, f0, fw):
+        def out_gather(gi, f0, fw, split=0):
             quads = work.tile([P, fw, 4], BF16, name="out_quads", tag="quads", bufs=4, align_bytes=64)
             out_quads[gi, f0] = quads
-            nc.vector.tensor_copy(out=quads[:], in_=out_wide[gi, f0][:].rearrange("p t f -> p f t"))
+            wide = out_wide[gi, f0][:].rearrange("p t f -> p f t")
+            nc.vector.tensor_copy(out=quads[:, split:fw, :], in_=wide[:, split:fw, :])
+            if split:
+                nc.scalar.copy(out=quads[:, 0:split, :], in_=wide[:, 0:split, :])
 
         def out_quantize(gi, f0, fw):
             if f0 == 0:
@@ -453,52 +487,62 @@ def tile_sinkhorninverseotresidualpull_x1_kernel(tc, q, k, a, t, g, v, out_0, ou
             )
             if f0 + fw == F:
                 for Q in range(4):
-                    nc.sync.dma_start(
+                    (nc.scalar if gi == 1 and Q > 1 else nc.sync).dma_start(
                         out=out_2[gi, 4 * Q : 4 * Q + 4, :].bitcast(I32),
                         in_=out_scales[gi][32 * Q : 32 * Q + 4, :].bitcast(I32),
                     )
 
+        for s in range(4):
+            pull_bank(0, 0, s, "x")
+            keep_clock(out_banks[0, 0, s])
         for u in range(2):
-            turn_t(1, 1, u)
+            turn_t(1, 1, u, 2)
         for J in range(4, 8):
             gain_scalar(J, 0)
+        for J in range(4):
+            if J == 3:
+                col_residual(3, 1)
+            gain_scalar(J, 1)
         quantize_r(0, 0)
         for s in range(4):
-            pull_open(0, 0, s, "x")
-        col_residual(3, 1)
-        gain_gather(1, 0)
-        for J in range(4):
-            gain_scalar(J, 1)
+            pull_open(0, 0, s)
+        gain_gather(1, 0, 0, 256)
+        quantize_r(1, 0, 0, 256)
+        gain_gather(1, 0, 256, W)
+        pull_close(0, 0, 0, s_out)
+        pull_close(0, 0, 1, s_out)
         col_residual(4, 1)
-        quantize_r(1, 0)
-        for J in range(5, 8):
+        quantize_r(1, 0, 256, W)
+        gain_scalar(4, 1)
+        for J in (5, 6):
             col_residual(J, 1)
-        gain_gather(0, 1)
-
+            gain_scalar(J, 1)
+        pull_close(0, 0, 2, s_out)
+        col_residual(7, 1)
+        gain_scalar(7, 1)
+        pull_close(0, 0, 3, s_out)
+        gain_gather(0, 1, 0, W)
         for s in range(4):
-            pull_close(0, 0, s, s_out)
-            gain_scalar(4 + s, 1)
-        quantize_v(1)
-        quantize_v(3)
-        for s in range(4):
-            pull_open(0, W, s, "x")
-        quantize_r(0, 1)
-        gain_gather(1, 1)
+            pull_bank(0, W, s, "y")
+            pull_open(0, W, s)
         for s in range(4):
             pull_close(0, W, s, s_out)
+        quantize_r(0, 1)
+        gain_gather(1, 1, 0, W)
         for s in range(4):
-            pull_open(1, 0, s, "y")
-        out_gather(0, 0, W)
+            pull_bank(1, 0, s, "x")
+            pull_open(1, 0, s)
         quantize_r(1, 1)
+        out_gather(0, 0, W)
         out_quantize(0, 0, W)
         for s in range(4):
             pull_close(1, 0, s, s_out)
-        out_gather(0, W, W)
+        out_gather(0, W, W, 256)
         for f0 in (W, 768):
             for s in (0, 2):
-                pull_quarter(1, f0, s, "x", s_out)
-        out_quantize(0, W, W)
+                pull_quarter(1, f0, s, "y", s_out)
         out_gather(1, 0, W)
+        out_quantize(0, W, W)
         out_gather(1, W, 256)
         out_quantize(1, 0, W)
         out_gather(1, 768, 256)

@@ -54,8 +54,6 @@ def tile_sinkhorninverseotresidualpull_x1_kernel(tc, q, k, a, t, g, v, out_0, ou
             for G in range(2):
                 nc.sync.dma_start(out=dst[G][:], in_=src[W * G : W * G + W, :].rearrange("(p t) d -> p t d", t=4))
 
-        zeros = keep.tile([P, P], F32, name="zeros")
-        nc.vector.memset(zeros[:], 0.0)
         ident = keep.tile([P, P], F32, name="ident")
         make_identity(nc, ident[:])
         warm = keep.tile([P, 2], F32, name="warm")
@@ -76,9 +74,6 @@ def tile_sinkhorninverseotresidualpull_x1_kernel(tc, q, k, a, t, g, v, out_0, ou
 
         def bank_pair(tag):
             return [bank(tag), bank(tag)]
-
-        def keep_clock(b):
-            nc.tensor.matmul(b[:, 0:P], lhsT=zeros[:], rhs=zeros[:], start=True, stop=True)
 
         def quad_tile(name):
             return work.tile([P, W, 4], BF16, name=name, tag="quads", bufs=4, align_bytes=64)
@@ -137,16 +132,15 @@ def tile_sinkhorninverseotresidualpull_x1_kernel(tc, q, k, a, t, g, v, out_0, ou
         z2 = keep.tile([P, 8, 2], F32, name="z2")
         ps = {}
 
-        def score(n, h, times=1):
+        def score(n, h):
             if h == 0:
                 ps[n] = bank_pair(TAGS[n // 2 % 2])
-            for i in range(times):
-                nc.tensor.matmul_mx(
-                    out=ps[n][h][:],
-                    lhsT=q_codes[:, P * n : P * n + P].bitcast(FP8X4), lhsT_scale=q_scales[:, P * n : P * n + P],
-                    rhs=k_codes[:, W * h : W * h + W].bitcast(FP8X4), rhs_scale=k_scales[:, W * h : W * h + W],
-                    start=True, stop=True,
-                )
+            nc.tensor.matmul_mx(
+                out=ps[n][h][:],
+                lhsT=q_codes[:, P * n : P * n + P].bitcast(FP8X4), lhsT_scale=q_scales[:, P * n : P * n + P],
+                rhs=k_codes[:, W * h : W * h + W].bitcast(FP8X4), rhs_scale=k_scales[:, W * h : W * h + W],
+                start=True, stop=True,
+            )
 
         def half_max(n, h):
             nc.vector.reduce_max(out=maxes[:, n, h : h + 1], in_=ps[n][h][:], axis=AX.X)
@@ -169,21 +163,14 @@ def tile_sinkhorninverseotresidualpull_x1_kernel(tc, q, k, a, t, g, v, out_0, ou
         for name, tag in (("k0", "x"), ("k1", "x"), ("q0", "y"), ("q1", "y")):
             for c in range(2):
                 turned[name, c] = bank(tag)
-        for b in (("k0", 0), ("k0", 1), ("k1", 0), ("k1", 1), ("q0", 0)):
-            keep_clock(turned[b])
         turn_rows(k_raw[0], kq[0], turned["k0", 0], 0, s_copy)
-        keep_clock(turned["q0", 1])
         turn_rows(k_raw[0], kq[0], turned["k0", 1], 1, v_copy)
-        keep_clock(turned["q1", 0])
         turn_rows(q_raw[0], qq[0], turned["q0", 0], 0, s_copy)
-        keep_clock(turned["q1", 1])
         quantize_k(0)
         quantize_q(0, 0)
         turn_rows(k_raw[1], kq[1], turned["k1", 0], 0, s_copy)
-        keep_clock(turned["q1", 1])
         turn_rows(k_raw[1], kq[1], turned["k1", 1], 1, v_copy)
         quantize_k(1)
-        keep_clock(turned["q1", 1])
         turn_rows(q_raw[0], qq[0], turned["q0", 1], 1, s_copy)
         score(0, 0)
         half_max(0, 0)
@@ -214,7 +201,7 @@ def tile_sinkhorninverseotresidualpull_x1_kernel(tc, q, k, a, t, g, v, out_0, ou
                 quantize_q(1, 0)
             if n == 3:
                 quantize_q(1, 1)
-                for i in range(4):
+                for i in (0, 2, 1, 3):
                     gather_v(i)
         row_shift(7)
         row_exp(7)
@@ -255,7 +242,7 @@ def tile_sinkhorninverseotresidualpull_x1_kernel(tc, q, k, a, t, g, v, out_0, ou
         nc.vector.tensor_scalar(out=a_raw[:], in0=a_shift[:], scalar1=RAW, scalar2=None, op0=ALU.mult)
         for n in range(8):
             for h in range(2):
-                score(n, h, 2 if n > 5 else 1)
+                score(n, h)
             if n == 1:
                 nc.vector.tensor_tensor(out=z[:], in0=z2[:, :, 0], in1=z2[:, :, 1], op=ALU.add)
                 nc.scalar.activation(out=ln_z[:], in_=z[:], func=ACT.Ln)
@@ -275,8 +262,6 @@ def tile_sinkhorninverseotresidualpull_x1_kernel(tc, q, k, a, t, g, v, out_0, ou
         b_vector(7, 0)
         b_vector(7, 1)
         pair = bank_pair("x")
-        keep_clock(pair[0])
-        keep_clock(pair[0])
         for J in range(8):
             nc.tensor.transpose(
                 pair[J // 4][:, P * (J % 4) : P * (J % 4) + P], acc[J // 4][:, P * (J % 4) : P * (J % 4) + P], ident[:]
@@ -291,11 +276,9 @@ def tile_sinkhorninverseotresidualpull_x1_kernel(tc, q, k, a, t, g, v, out_0, ou
 
         t_pair = {}
 
-        def turn_t(G, gi, u, clock=0):
+        def turn_t(G, gi, u):
             xt = bank("y")
             t_pair[G, gi, u] = xt
-            for i in range(clock):
-                keep_clock(xt)
             for s in range(4):
                 words = t_raw[gi][:, s, :].bitcast(F32)
                 nc.tensor.transpose(xt[:, P * s : P * s + P], words[:, 256 * G + u : 256 * G + 256 : 2], ident[:])
@@ -311,8 +294,6 @@ def tile_sinkhorninverseotresidualpull_x1_kernel(tc, q, k, a, t, g, v, out_0, ou
             e_cols[J] = work.tile([P, 2, W], F32, name="e_cols", tag="e_cols", bufs=8)
             pair = bank_pair("x")
             for gi in range(2):
-                if gi == 0 or J % 2 == 0:
-                    keep_clock(pair[gi])
                 for s in range(4):
                     nc.tensor.transpose(
                         pair[gi][:, P * s : P * s + P],
@@ -328,15 +309,9 @@ def tile_sinkhorninverseotresidualpull_x1_kernel(tc, q, k, a, t, g, v, out_0, ou
                 )
 
         def col_sum(J):
-            if J not in S_SUM:
-                nc.vector.tensor_scalar(
-                    out=ezs[:, J : J + 1], in0=ez[:, J, 0:1], scalar1=ez[:, J, 1:2], scalar2=1.0 / M,
-                    op0=ALU.add, op1=ALU.mult,
-                )
-                return
-            both = keep.tile([P, 2], F32, name="both" + str(J))
-            nc.scalar.activation(
-                out=both[:], in_=ez[:, J, :], func=ACT.Copy, scale=1.0 / M, accum_out=ezs[:, J : J + 1],
+            nc.vector.tensor_scalar(
+                out=ezs[:, J : J + 1], in0=ez[:, J, 0:1], scalar1=ez[:, J, 1:2], scalar2=1.0 / M,
+                op0=ALU.add, op1=ALU.mult,
             )
 
         def col_weight(J):
@@ -392,13 +367,10 @@ def tile_sinkhorninverseotresidualpull_x1_kernel(tc, q, k, a, t, g, v, out_0, ou
         turn_t(0, 0, 1)
         col_exp(0)
         FILL = {4: 0, 5: 1, 6: 2}
-        S_SUM = (4, 5, 6)
         for J in range(8):
             if J < 7:
-                col_exp(J + 1, (0,))
+                col_exp(J + 1)
             col_sum(J)
-            if J < 7:
-                col_exp(J + 1, (1,))
             if J < 6:
                 turn_b(J + 2)
             if J in (0, 1):
@@ -408,8 +380,8 @@ def tile_sinkhorninverseotresidualpull_x1_kernel(tc, q, k, a, t, g, v, out_0, ou
             col_weight(J)
             if J in FILL:
                 col_residual(FILL[J], 1)
-            if J in (1, 2):
-                quantize_v(2 * J - 1)
+            if J in (2, 3):
+                quantize_v(2 * J - 3)
             col_residual(J, 0)
             if J == 3:
                 new_quads(0, 0)
@@ -465,13 +437,10 @@ def tile_sinkhorninverseotresidualpull_x1_kernel(tc, q, k, a, t, g, v, out_0, ou
         def s_out(dst, src):
             nc.scalar.activation(out=dst, in_=src, func=ACT.Copy, scale=PULL)
 
-        def out_gather(gi, f0, fw, split=0):
+        def out_gather(gi, f0, fw):
             quads = work.tile([P, fw, 4], BF16, name="out_quads", tag="quads", bufs=4, align_bytes=64)
             out_quads[gi, f0] = quads
-            wide = out_wide[gi, f0][:].rearrange("p t f -> p f t")
-            nc.vector.tensor_copy(out=quads[:, split:fw, :], in_=wide[:, split:fw, :])
-            if split:
-                nc.scalar.copy(out=quads[:, 0:split, :], in_=wide[:, 0:split, :])
+            nc.vector.tensor_copy(out=quads[:], in_=out_wide[gi, f0][:].rearrange("p t f -> p f t"))
 
         def out_quantize(gi, f0, fw):
             if f0 == 0:
@@ -494,9 +463,8 @@ def tile_sinkhorninverseotresidualpull_x1_kernel(tc, q, k, a, t, g, v, out_0, ou
 
         for s in range(4):
             pull_bank(0, 0, s, "x")
-            keep_clock(out_banks[0, 0, s])
         for u in range(2):
-            turn_t(1, 1, u, 2)
+            turn_t(1, 1, u)
         for J in range(4, 8):
             gain_scalar(J, 0)
         for J in range(4):
@@ -537,7 +505,7 @@ def tile_sinkhorninverseotresidualpull_x1_kernel(tc, q, k, a, t, g, v, out_0, ou
         out_quantize(0, 0, W)
         for s in range(4):
             pull_close(1, 0, s, s_out)
-        out_gather(0, W, W, 256)
+        out_gather(0, W, W)
         for f0 in (W, 768):
             for s in (0, 2):
                 pull_quarter(1, f0, s, "y", s_out)

import math
from contextlib import ExitStack

import concourse.mybir as mybir
from concourse.masks import make_identity

N, M, D, F = 1024, 1024, 512, 1024
FLOPS = 2 * N * M * D + 2 * N * M * F

F32 = mybir.dt.float32
BF16 = mybir.dt.bfloat16
U32 = mybir.dt.uint32
I32 = mybir.dt.int32
U8 = mybir.dt.uint8
FP8X4 = mybir.dt.float8_e4m3fn_x4
ALU = mybir.AluOpType
ACT = mybir.ActivationFunctionType
AX = mybir.AxisListType

P = 128
W = 512
SCALE = 1.0 / math.sqrt(D)
RAW = math.sqrt(D)
PULL = 1.0 / math.sqrt(M)


def tile_sinkhorninverseotresidualpull_x1_kernel(tc, q, k, a, t, g, v, out_0, out_1, out_2):
    nc = tc.nc
    with ExitStack() as ctx:
        keep = ctx.enter_context(tc.tile_pool(name="keep", bufs=1))
        work = ctx.enter_context(tc.tile_pool(name="work", bufs=4))
        psum = ctx.enter_context(tc.psum_pool(name="psum", bufs=4))
        ctx.enter_context(tc.manual_schedule())

        k_raw = [keep.tile([P, 4, D], BF16, name="k_raw" + str(G)) for G in range(2)]
        q_raw = [keep.tile([P, 4, D], BF16, name="q_raw" + str(G)) for G in range(2)]
        v_raw = [keep.tile([P, 4, F], BF16, name="v_raw" + str(G)) for G in range(2)]
        t_raw = [keep.tile([P, 4, M], BF16, name="t_raw" + str(G)) for G in range(2)]

        def load_half(dst, src, G, c):
            rows = src[W * G : W * G + W, :].rearrange("(p t) d -> p t d", t=4)
            nc.sync.dma_start(out=dst[G][:, 2 * c : 2 * c + 2, :], in_=rows[:, 2 * c : 2 * c + 2, :])

        for dst, src, G, c in (
            (k_raw, k, 0, 0), (k_raw, k, 0, 1), (q_raw, q, 0, 0), (k_raw, k, 1, 0),
            (k_raw, k, 1, 1), (q_raw, q, 0, 1), (q_raw, q, 1, 0), (q_raw, q, 1, 1),
        ):
            load_half(dst, src, G, c)
        a_bf = keep.tile([P, 2, 4], BF16, name="a_bf")
        g_bf = keep.tile([P, 2, 4], BF16, name="g_bf")
        nc.sync.dma_start(out=a_bf[:], in_=a.rearrange("(g p t) -> p g t", g=2, t=4))
        nc.sync.dma_start(out=g_bf[:], in_=g.rearrange("(g p t) -> p g t", g=2, t=4))
        for dst, src in ((v_raw, v), (t_raw, t)):
            for G in range(2):
                nc.sync.dma_start(out=dst[G][:], in_=src[W * G : W * G + W, :].rearrange("(p t) d -> p t d", t=4))

        ident = keep.tile([P, P], F32, name="ident")
        make_identity(nc, ident[:])
        warm = keep.tile([P, 2], F32, name="warm")
        nc.vector.memset(warm[:], 0.0)
        nc.scalar.activation(out=warm[:, 1:2], in_=warm[:, 0:1], func=ACT.Exp)

        k_codes = keep.tile([P, M], U32, name="k_codes", align_bytes=64)
        k_scales = keep.tile([P, M], U8, name="k_scales", align_bytes=64)
        q_codes = keep.tile([P, N], U32, name="q_codes", align_bytes=64)
        q_scales = keep.tile([P, N], U8, name="q_scales", align_bytes=64)
        v_codes = [keep.tile([P, F], U32, name="v_codes" + str(G), align_bytes=64) for G in range(2)]
        v_scales = [keep.tile([P, F], U8, name="v_scales" + str(G), align_bytes=64) for G in range(2)]
        r_codes = [keep.tile([P, N], U32, name="r_codes" + str(G), align_bytes=64) for G in range(2)]
        r_scales = [keep.tile([P, N], U8, name="r_scales" + str(G), align_bytes=64) for G in range(2)]

        def bank(tag):
            return psum.tile([P, W], F32, name="bank_" + tag, tag=tag)

        def bank_pair(tag):
            return [bank(tag), bank(tag)]

        def quad_tile(name):
            return work.tile([P, W, 4], BF16, name=name, tag="quads", bufs=4, align_bytes=64)

        def quantize(quads, codes, scales, cols):
            nc.vector.quantize_mx(
                out=codes[:, cols].bitcast(FP8X4),
                scales=scales[:, cols],
                in_=quads.rearrange("p c t -> p (c t)"),
            )

        def turn_rows(raw, quads, b, c, copy):
            words = raw[:].bitcast(F32)
            xt = b[:].rearrange("p (s u r) -> p s u r", s=2, u=2)
            for s in range(2):
                for u in range(2):
                    nc.tensor.transpose(xt[:, s, u, :], words[:, 2 * c + s, u : D // 2 : 2], ident[:])
            dst = quads[:, 256 * c : 256 * (c + 1), :].bitcast(F32).rearrange("p (s r) u -> p s r u", s=2)
            copy(dst, xt.rearrange("p s u r -> p s r u"))

        def s_copy(dst, src):
            nc.scalar.copy(out=dst, in_=src)

        def v_copy(dst, src):
            nc.vector.tensor_copy(out=dst, in_=src)

        qq1 = quad_tile("q_quads")
        kq = [quad_tile("k_quads") for G in range(2)]
        qq = [quad_tile("q_quads"), qq1]

        def quantize_k(G):
            quantize(kq[G][:], k_codes, k_scales, slice(W * G, W * G + W))

        def quantize_q(G, c):
            quantize(qq[G][:, 256 * c : 256 * c + 256, :], q_codes, q_scales, slice(W * G + 256 * c, W * G + 256 * c + 256))

        v_quads = {}

        def gather_v(i):
            G, c = divmod(i, 2)
            v_quads[i] = quad_tile("v_quads")
            for lo in range(0, W, 128):
                nc.gpsimd.tensor_scalar(
                    out=v_quads[i][:, lo : lo + 128, :],
                    in0=v_raw[G][:, :, W * c + lo : W * c + lo + 128].rearrange("p t f -> p f t"),
                    scalar1=1.0, scalar2=0.0, op0=ALU.mult, op1=ALU.add,
                )

        def quantize_v(i):
            G, c = divmod(i, 2)
            quantize(v_quads[i][:], v_codes[G], v_scales[G], slice(W * c, W * c + W))

        TAGS = ("x", "y")
        maxes = keep.tile([P, 8, 2], F32, name="maxes")
        shift = keep.tile([P, 8], F32, name="shift")
        z2 = keep.tile([P, 8, 2], F32, name="z2")
        ps = {}

        def score(n, h):
            if h == 0:
                ps[n] = bank_pair(TAGS[n // 2 % 2])
            nc.tensor.matmul_mx(
                out=ps[n][h][:],
                lhsT=q_codes[:, P * n : P * n + P].bitcast(FP8X4), lhsT_scale=q_scales[:, P * n : P * n + P],
                rhs=k_codes[:, W * h : W * h + W].bitcast(FP8X4), rhs_scale=k_scales[:, W * h : W * h + W],
                start=True, stop=True,
            )

        def half_max(n, h):
            nc.vector.reduce_max(out=maxes[:, n, h : h + 1], in_=ps[n][h][:], axis=AX.X)

        def row_shift(n):
            nc.vector.tensor_scalar(
                out=shift[:, n : n + 1], in0=maxes[:, n, 0:1], scalar1=maxes[:, n, 1:2], scalar2=-SCALE,
                op0=ALU.max, op1=ALU.mult,
            )

        def row_exp(n):
            for h in range(2):
                junk = work.tile([P, W], BF16, name="junk", tag="junk", bufs=2)
                nc.scalar.activation(
                    out=junk[:], in_=ps[n][h][:], func=ACT.Exp, bias=shift[:, n : n + 1], scale=SCALE,
                    accum_out=z2[:, n, h : h + 1],
                )

        turned = {}
        for name, tag in (("k0", "x"), ("k1", "x"), ("q0", "y"), ("q1", "y")):
            for c in range(2):
                turned[name, c] = bank(tag)
        turn_rows(k_raw[0], kq[0], turned["k0", 0], 0, s_copy)
        turn_rows(k_raw[0], kq[0], turned["k0", 1], 1, v_copy)
        turn_rows(q_raw[0], qq[0], turned["q0", 0], 0, s_copy)
        quantize_k(0)
        quantize_q(0, 0)
        turn_rows(k_raw[1], kq[1], turned["k1", 0], 0, s_copy)
        turn_rows(k_raw[1], kq[1], turned["k1", 1], 1, v_copy)
        quantize_k(1)
        turn_rows(q_raw[0], qq[0], turned["q0", 1], 1, s_copy)
        score(0, 0)
        half_max(0, 0)
        turn_rows(q_raw[1], qq[1], turned["q1", 0], 0, s_copy)
        score(0, 1)
        score(1, 0)
        score(1, 1)
        half_max(0, 1)
        row_shift(0)
        quantize_q(0, 1)
        turn_rows(q_raw[1], qq[1], turned["q1", 1], 1, s_copy)
        row_exp(0)
        half_max(1, 0)
        half_max(1, 1)
        row_shift(1)
        row_exp(1)
        for n in range(2, 8):
            score(n, 0)
            score(n, 1)
            half_max(n, 0)
            if n > 3:
                row_shift(n - 1)
                row_exp(n - 1)
            half_max(n, 1)
            if n == 2:
                row_shift(n)
                row_exp(n)
                quantize_q(1, 0)
            if n == 3:
                quantize_q(1, 1)
                for i in (0, 2, 1, 3):
                    gather_v(i)
        row_shift(7)
        row_exp(7)
        g_f32 = keep.tile([P, 2, 1, 4], F32, name="g_f32")
        nc.vector.tensor_copy(out=g_f32[:, :, 0, :], in_=g_bf[:])

        a_shift = keep.tile([P, 8], F32, name="a_shift")
        a_raw = keep.tile([P, 8], F32, name="a_raw")
        ln_z = keep.tile([P, 8], F32, name="ln_z")
        c_row = keep.tile([P, 8], F32, name="c_row")
        z = keep.tile([P, 8], F32, name="z")
        b_rows = [keep.tile([P, 2, W], F32, name="b_rows" + str(n)) for n in range(8)]
        acc = [keep.tile([P, W], F32, name="acc" + str(h)) for h in range(2)]

        def b_scalar(n, h):
            nc.scalar.activation(
                out=b_rows[n][:, h, :], in_=ps[n][h][:], func=ACT.Identity, bias=c_row[:, n : n + 1], scale=SCALE,
            )

        def b_vector(n, h):
            nc.vector.tensor_scalar(
                out=b_rows[n][:, h, :], in0=ps[n][h][:], scalar1=SCALE, scalar2=c_row[:, n : n + 1],
                op0=ALU.mult, op1=ALU.add,
            )

        def col_max(n, h):
            if n == 0:
                nc.vector.tensor_scalar(
                    out=acc[h][:], in0=ps[n][h][:], scalar1=a_raw[:, 0:1], scalar2=None, op0=ALU.add
                )
            else:
                nc.vector.scalar_tensor_tensor(
                    out=acc[h][:], in0=ps[n][h][:], scalar=a_raw[:, n : n + 1], in1=acc[h][:],
                    op0=ALU.add, op1=ALU.max,
                )

        nc.vector.tensor_tensor(out=a_shift[:], in0=a_bf[:].rearrange("p g t -> p (g t)"), in1=shift[:], op=ALU.add)
        nc.vector.tensor_scalar(out=a_raw[:], in0=a_shift[:], scalar1=RAW, scalar2=None, op0=ALU.mult)
        for n in range(8):
            for h in range(2):
                score(n, h)
            if n == 1:
                nc.vector.tensor_tensor(out=z[:], in0=z2[:, :, 0], in1=z2[:, :, 1], op=ALU.add)
                nc.scalar.activation(out=ln_z[:], in_=z[:], func=ACT.Ln)
            col_max(n, 0)
            if n == 2:
                nc.vector.tensor_tensor(out=c_row[:], in0=a_shift[:], in1=ln_z[:], op=ALU.subtract)
                for m in range(2):
                    for h in range(2):
                        b_scalar(m, h)
            col_max(n, 1)
            if 2 <= n < 7:
                for h in range(2 if n < 6 else 1):
                    b_scalar(n, h)
        h_raw = keep.tile([P, 8], F32, name="h_raw")
        h_shift = keep.tile([P, 8], F32, name="h_shift")
        b_vector(6, 1)
        b_vector(7, 0)
        b_vector(7, 1)
        pair = bank_pair("x")
        for J in range(8):
            nc.tensor.transpose(
                pair[J // 4][:, P * (J % 4) : P * (J % 4) + P], acc[J // 4][:, P * (J % 4) : P * (J % 4) + P], ident[:]
            )
        for h in range(2):
            nc.vector.reduce_max(
                out=h_raw[:, 4 * h : 4 * h + 4], in_=pair[h][:].rearrange("p (c r) -> p c r", c=4), axis=AX.X
            )
        nc.vector.tensor_scalar(out=h_shift[:], in0=h_raw[:], scalar1=-SCALE, scalar2=None, op0=ALU.mult)
        quantize_v(0)
        quantize_v(2)

        t_pair = {}

        def turn_t(G, gi, u):
            xt = bank("y")
            t_pair[G, gi, u] = xt
            for s in range(4):
                words = t_raw[gi][:, s, :].bitcast(F32)
                nc.tensor.transpose(xt[:, P * s : P * s + P], words[:, 256 * G + u : 256 * G + 256 : 2], ident[:])

        e_cols = {}
        ez = keep.tile([P, 8, 2], F32, name="ez")
        ezs = keep.tile([P, 8], F32, name="ezs")
        w_col = keep.tile([P, 8], F32, name="w_col")

        e_pair = {}

        def turn_b(J):
            e_cols[J] = work.tile([P, 2, W], F32, name="e_cols", tag="e_cols", bufs=8)
            pair = bank_pair("x")
            for gi in range(2):
                for s in range(4):
                    nc.tensor.transpose(
                        pair[gi][:, P * s : P * s + P],
                        b_rows[4 * gi + s][:, J // 4, P * (J % 4) : P * (J % 4) + P], ident[:]
                    )
            e_pair[J] = pair

        def col_exp(J, halves=(0, 1)):
            for gi in halves:
                nc.scalar.activation(
                    out=e_cols[J][:, gi, :], in_=e_pair[J][gi][:], func=ACT.Exp, bias=h_shift[:, J : J + 1],
                    accum_out=ez[:, J, gi : gi + 1],
                )

        def col_sum(J):
            nc.vector.tensor_scalar(
                out=ezs[:, J : J + 1], in0=ez[:, J, 0:1], scalar1=ez[:, J, 1:2], scalar2=1.0 / M,
                op0=ALU.add, op1=ALU.mult,
            )

        def col_weight(J):
            nc.vector.reciprocal(out=w_col[:, J : J + 1], in_=ezs[:, J : J + 1])

        residual = {}
        r_quads = {}
        gained = {}

        def col_residual(J, gi):
            G, s = divmod(J, 4)
            if s == 0:
                residual[G, gi] = work.tile([P, 4, W], F32, name="residual", tag="wide", bufs=4)
            u, e = divmod(s, 2)
            t_view = t_pair[G, gi, u][:].bitcast(BF16).rearrange("p (i e) -> p i e", e=2)[:, :, e]
            nc.vector.scalar_tensor_tensor(
                out=residual[G, gi][:, s, :], in0=e_cols[J][:, gi, :], scalar=w_col[:, J : J + 1],
                in1=t_view, op0=ALU.mult, op1=ALU.subtract,
            )

        def new_quads(G, gi):
            r_quads[G, gi] = quad_tile("r_quads")

        def gain_pool(G, gi, lo, hi):
            nc.gpsimd.tensor_tensor(
                out=r_quads[G, gi][:, lo:hi, :],
                in0=residual[G, gi][:].rearrange("p t i -> p i t")[:, lo:hi, :],
                in1=g_f32[:, G, :, :].to_broadcast([P, hi - lo, 4]), op=ALU.mult,
            )

        def gain_scalar(J, gi):
            G, s = divmod(J, 4)
            if s == 0:
                gained[G, gi] = work.tile([P, 4, W], BF16, name="gained", tag="gained", bufs=2)
            nc.scalar.activation(
                out=gained[G, gi][:, s, :], in_=residual[G, gi][:, s, :], func=ACT.Copy,
                scale=g_f32[:, G, 0, s : s + 1],
            )

        def gain_gather(G, gi, lo, hi):
            if lo == 0:
                new_quads(G, gi)
            nc.vector.tensor_copy(
                out=r_quads[G, gi][:, lo:hi, :], in_=gained[G, gi][:].rearrange("p t i -> p i t")[:, lo:hi, :]
            )

        def quantize_r(G, gi, lo=0, hi=W):
            quantize(r_quads[G, gi][:, lo:hi, :], r_codes[G], r_scales[G], slice(W * gi + lo, W * gi + hi))

        turn_b(0)
        turn_t(0, 0, 0)
        turn_b(1)
        turn_t(0, 0, 1)
        col_exp(0)
        FILL = {4: 0, 5: 1, 6: 2}
        for J in range(8):
            if J < 7:
                col_exp(J + 1)
            col_sum(J)
            if J < 6:
                turn_b(J + 2)
            if J in (0, 1):
                turn_t(1, 0, J)
            if J in (2, 4):
                turn_t(0, 1, J // 2 - 1)
            col_weight(J)
            if J in FILL:
                col_residual(FILL[J], 1)
            if J in (2, 3):
                quantize_v(2 * J - 3)
            col_residual(J, 0)
            if J == 3:
                new_quads(0, 0)
                for lo in range(0, W, 64):
                    gain_pool(0, 0, lo, lo + 64)

        out_wide = {}
        out_quads = {}
        out_scales = {}

        out_banks = {}

        def pull_bank(gi, f0, s, tag):
            out_banks[gi, f0, s] = bank(tag)

        def pull_open(gi, f0, s):
            pull_pass(gi, f0, W, s, 0, out_banks[gi, f0, s][:])

        def pull_pass(gi, f0, fw, s, G, dst):
            cols = slice(W * gi + P * s, W * gi + P * s + P)
            f_cols = slice(f0, f0 + fw)
            nc.tensor.matmul_mx(
                out=dst,
                lhsT=r_codes[G][:, cols].bitcast(FP8X4), lhsT_scale=r_scales[G][:, cols],
                rhs=v_codes[G][:, f_cols].bitcast(FP8X4), rhs_scale=v_scales[G][:, f_cols],
                start=(G == 0), stop=(G == 1),
            )

        def store_rows(gi, f0, fw, s):
            nc.sync.dma_start(
                out=out_0[W * gi : W * gi + W, :].rearrange("(p t) f -> p t f", t=4)[:, s : s + 2, f0 : f0 + fw],
                in_=out_wide[gi, f0][:, s : s + 2, :],
            )

        def pull_close(gi, f0, s, copy):
            if s == 0:
                out_wide[gi, f0] = work.tile([P, 4, W], F32, name="out_wide", tag="wide", bufs=4)
            pull_pass(gi, f0, W, s, 1, out_banks[gi, f0, s][:])
            copy(out_wide[gi, f0][:, s, :], out_banks[gi, f0, s][:])
            if s % 2 == 1:
                store_rows(gi, f0, W, s - 1)

        def pull_quarter(gi, f0, s, tag, copy):
            if s == 0:
                out_wide[gi, f0] = work.tile([P, 4, 256], F32, name="out_wide", tag="wide", bufs=4)
            xt = bank(tag)
            for c in range(2):
                for G in range(2):
                    pull_pass(gi, f0, 256, s + c, G, xt[:, 256 * c : 256 * c + 256])
            copy(out_wide[gi, f0][:, s : s + 2, :], xt[:].rearrange("p (t f) -> p t f", t=2))
            store_rows(gi, f0, 256, s)

        def s_out(dst, src):
            nc.scalar.activation(out=dst, in_=src, func=ACT.Copy, scale=PULL)

        def out_gather(gi, f0, fw):
            quads = work.tile([P, fw, 4], BF16, name="out_quads", tag="quads", bufs=4, align_bytes=64)
            out_quads[gi, f0] = quads
            nc.vector.tensor_copy(out=quads[:], in_=out_wide[gi, f0][:].rearrange("p t f -> p f t"))

        def out_quantize(gi, f0, fw):
            if f0 == 0:
                out_scales[gi] = keep.tile([P, F], U8, name="out_scales" + str(gi), align_bytes=64)
            codes = work.tile([P, fw], U32, name="out_codes", tag="out_codes", bufs=5, align_bytes=64)
            nc.vector.quantize_mx(
                out=codes[:].bitcast(FP8X4), scales=out_scales[gi][:, f0 : f0 + fw],
                in_=out_quads[gi, f0][:].rearrange("p f t -> p (f t)"),
            )
            nc.sync.dma_start(
                out=out_1[gi].rearrange("p f t -> p (f t)")[:, 4 * f0 : 4 * (f0 + fw)].bitcast(I32),
                in_=codes[:].bitcast(I32),
            )
            if f0 + fw == F:
                for Q in range(4):
                    (nc.scalar if gi == 1 and Q > 1 else nc.sync).dma_start(
                        out=out_2[gi, 4 * Q : 4 * Q + 4, :].bitcast(I32),
                        in_=out_scales[gi][32 * Q : 32 * Q + 4, :].bitcast(I32),
                    )

        for s in range(4):
            pull_bank(0, 0, s, "x")
        for u in range(2):
            turn_t(1, 1, u)
        for J in range(4, 8):
            gain_scalar(J, 0)
        for J in range(4):
            if J == 3:
                col_residual(3, 1)
            gain_scalar(J, 1)
        quantize_r(0, 0)
        for s in range(4):
            pull_open(0, 0, s)
        gain_gather(1, 0, 0, 256)
        quantize_r(1, 0, 0, 256)
        gain_gather(1, 0, 256, W)
        pull_close(0, 0, 0, s_out)
        pull_close(0, 0, 1, s_out)
        col_residual(4, 1)
        quantize_r(1, 0, 256, W)
        gain_scalar(4, 1)
        for J in (5, 6):
            col_residual(J, 1)
            gain_scalar(J, 1)
        pull_close(0, 0, 2, s_out)
        col_residual(7, 1)
        gain_scalar(7, 1)
        pull_close(0, 0, 3, s_out)
        gain_gather(0, 1, 0, W)
        for s in range(4):
            pull_bank(0, W, s, "y")
            pull_open(0, W, s)
        for s in range(4):
            pull_close(0, W, s, s_out)
        quantize_r(0, 1)
        gain_gather(1, 1, 0, W)
        for s in range(4):
            pull_bank(1, 0, s, "x")
            pull_open(1, 0, s)
        quantize_r(1, 1)
        out_gather(0, 0, W)
        out_quantize(0, 0, W)
        for s in range(4):
            pull_close(1, 0, s, s_out)
        out_gather(0, W, W)
        for f0 in (W, 768):
            for s in (0, 2):
                pull_quarter(1, f0, s, "y", s_out)
        out_gather(1, 0, W)
        out_quantize(0, W, W)
        out_gather(1, W, 256)
        out_quantize(1, 0, W)
        out_gather(1, 768, 256)
        out_quantize(1, W, 256)
        out_quantize(1, 768, 256)
